import numpy as np
import ml_dtypes


def mxq(x, axis, fmt="e4m3"):
    dtype, down = {"e4m3": (ml_dtypes.float8_e4m3fn, 7), "e5m2": (ml_dtypes.float8_e5m2, 14)}[fmt]
    v = np.moveaxis(np.asarray(x, np.float32).astype(ml_dtypes.bfloat16).astype(np.float64), axis, -1)
    blocks = v.reshape(v.shape[:-1] + (-1, 32))
    amax = np.abs(blocks).max(-1, keepdims=True)
    byte = np.maximum(np.where(amax > 0, np.frexp(amax)[1] - 1 + 127, 0) - down, 1)
    scale = np.exp2(byte - 127.0)
    codes = (blocks / scale).astype(np.float32).astype(dtype).astype(np.float64)
    return np.moveaxis((codes * scale).reshape(v.shape), -1, axis)


WIDE = False


def mx_kscale(k):
    if not WIDE:
        return np.ones(k)
    levels = np.array([30, -30])
    if k % 512:
        return np.exp2(np.random.permutation(np.resize(levels, k // 32))).repeat(32)
    a = np.empty((k // 512, 16))
    for p in range(k // 512):
        a[p, :8] = np.random.permutation(np.resize(levels, 8))
        for g in range(8):
            far = levels[np.abs(levels - a[p, g]) >= 10]
            a[p, g + 8] = far[np.random.randint(len(far))]
    return np.exp2(a.ravel()).repeat(32)


def f64(x):
    return np.asarray(x).astype(np.float64)


def striped8(idx):
    return np.concatenate([v.reshape(-1, 16).T for v in idx]).astype(np.uint16)


def unstriped8(offs):
    return np.stack([offs[16 * g:16 * g + 16].T.reshape(-1) for g in range(8)]).astype(np.int64)


E2M1 = np.array([0.0, 0.5, 1.0, 1.5, 2.0, 3.0, 4.0, 6.0, -0.0, -0.5, -1.0, -1.5, -2.0, -3.0, -4.0, -6.0])


def pack_weight(w, fmt):
    k, n = w.shape
    w = f64(np.asarray(w, np.float32).astype(ml_dtypes.bfloat16)).reshape(k // 32, 32, n)
    amax = np.abs(w).max(1)
    if fmt == "e4m3":
        byte = np.frexp(amax)[1] - 1 + 127 - 7
    else:
        mant, ex = np.frexp(amax / 6.0)
        byte = np.where(mant > 0.5, ex, ex - 1) + 127
    byte = np.clip(np.where(amax > 0, byte, 1), 1, 254)
    scaled = (w * np.exp2(127.0 - byte)[:, None, :]).reshape(k, n).astype(np.float32)
    by_word = np.ascontiguousarray(scaled.reshape(k // 512, 128, 4, n).transpose(0, 1, 3, 2))
    if fmt == "e4m3":
        words = by_word.astype(ml_dtypes.float8_e4m3fn).view(np.uint8)
    else:
        c = by_word.astype(ml_dtypes.float4_e2m1fn).view(np.uint8) & 0xF
        words = (c[..., 0::2] | (c[..., 1::2] << 4)).reshape(k // 512, 128, 2 * n)
    return np.ascontiguousarray(words), np.ascontiguousarray(byte.astype(np.uint8).reshape(k // 512, 16, n))


def unpack_weight(words, scales, fmt):
    g, _, n = scales.shape
    words = np.ascontiguousarray(words).reshape(g, 128, n, -1)
    if fmt == "e4m3":
        vals = words.view(ml_dtypes.float8_e4m3fn).astype(np.float64)
    else:
        nib = np.empty((g, 128, n, 4), np.uint8)
        nib[..., 0::2] = words & 0xF
        nib[..., 1::2] = words >> 4
        vals = E2M1[nib]
    vals = vals * np.repeat(np.exp2(scales.astype(np.float64) - 127.0), 8, axis=1)[..., None]
    return vals.transpose(0, 1, 3, 2).reshape(g * 512, n)


K, N, T, J = 1024, 512, 2048, 1024


def setup_inputs():
    n = np.random.standard_normal
    s = mx_kscale(K)[:, None]
    m = np.exp(0.5 * n((1, J)))
    w = n((K, N)) / np.sqrt(K) / s
    p_w8 = pack_weight(w[:512], "e4m3")
    p_w4 = pack_weight(w[512:], "e2m1")
    return {
        "dy": (m * n((K, J)) * s).astype(np.float32),
        "w8_words": p_w8[0],
        "w8_scales": p_w8[1],
        "w4_words": p_w4[0],
        "w4_scales": p_w4[1],
        "wgo": np.repeat(np.random.uniform(0.5, 2.0, (8, J)), 16, axis=0).astype(np.float32),
        "offs": striped8(np.stack([np.random.permutation(T)[:J] for _ in range(8)])),
    }


def reference(dy, w8_words, w8_scales, w4_words, w4_scales, wgo, offs):
    idx = unstriped8(offs)
    dy_ = mxq(f64(dy), 0, "e5m2")
    w8_ = unpack_weight(w8_words, w8_scales, "e4m3")
    w4_ = unpack_weight(w4_words, w4_scales, "e2m1")
    dx = w8_.T @ dy_[:512] + w4_.T @ dy_[512:]
    out = np.zeros((N, T))
    rows = np.arange(N)
    out[rows[:, None], idx[rows % 128 // 16]] = f64(wgo)[rows % 128] * (dx)
    return out

@@ -1,0 +1,177 @@
+from contextlib import ExitStack
+
+import concourse.mybir as mybir
+
+K, N, T, J = 1024, 512, 2048, 1024
+FLOPS = 2 * K * N * J
+
+F32 = mybir.dt.float32
+BF16 = mybir.dt.bfloat16
+I32 = mybir.dt.int32
+U32 = mybir.dt.uint32
+U16 = mybir.dt.uint16
+U8 = mybir.dt.uint8
+E4M3 = mybir.dt.float8_e4m3fn_x4
+E5M2 = mybir.dt.float8_e5m2_x4
+E2M1 = mybir.dt.float4_e2m1fn_x4
+MULT = mybir.AluOpType.mult
+
+P = 128
+PACK = 4
+K_PASS = P * PACK
+HALF = 512
+BLOCKS = N // P
+LIST_COLS = HALF // 16
+WINDOWS = 4
+
+
+def tile_list_embg_mix_none_kernel(tc, dy, w8_words, w8_scales, w4_words, w4_scales, wgo, offs, out):
+    nc = tc.nc
+    with ExitStack() as ctx:
+        keep = ctx.enter_context(tc.tile_pool(name="keep", bufs=1))
+        psum = ctx.enter_context(tc.psum_pool(name="psum", bufs=1))
+
+        offsets = keep.tile([P, J // 16], U16, name="offsets")
+        w_scales = keep.tile([P, 2 * N], U8, name="w_scales", align_bytes=64)
+        w8 = keep.tile([P, N], U32, name="w8", align_bytes=64)
+        w4 = keep.tile([P, 2 * N], U8, name="w4", align_bytes=64)
+        windows = [keep.tile([P, T], F32, name="window%d" % b) for b in range(2)]
+        gains = [keep.tile([P, HALF], F32, name="gain%d" % h) for h in range(2)]
+        raw = {}
+        grouped = {}
+        codes = {}
+        scales = {}
+        grouped_0 = keep.tile([P, 2, HALF, PACK], BF16, name="grouped0", tag="grouped0", align_bytes=64)
+        for h in range(2):
+            codes_h = keep.tile([P, 2, HALF], U32, name="codes%d" % h, tag="codes%d" % h, align_bytes=64)
+            scales_h = keep.tile([P, 2, HALF], U8, name="scales%d" % h, tag="scales%d" % h, align_bytes=64)
+            for a in range(2):
+                raw[h, a] = keep.tile([P, PACK, HALF], F32, name="raw%d%d" % (h, a))
+                codes[h, a] = codes_h[:, a]
+                scales[h, a] = scales_h[:, a]
+        for a in range(2):
+            grouped[0, a] = grouped_0[:, a]
+
+        w8_dram = w8_words[0].rearrange("p n t -> p (n t)").bitcast(I32)
+        w4_dram = w4_words[0].bitcast(I32)
+
+        def load_dy(h, a, c0, c1):
+            rows = dy[a * K_PASS : (a + 1) * K_PASS, h * HALF + c0 : h * HALF + c1]
+            nc.sync.dma_start(out=raw[h, a][:, :, c0:c1], in_=rows.rearrange("(p t) j -> p t j", t=PACK))
+
+        def load_w8(n0, n1):
+            nc.sync.dma_start(out=w8[:, n0:n1].bitcast(I32), in_=w8_dram[:, n0:n1])
+
+        def load_w4(n0, n1):
+            nc.sync.dma_start(out=w4[:, 2 * n0 : 2 * n1].bitcast(I32), in_=w4_dram[:, n0 // 2 : n1 // 2])
+
+        def load_scales(queue, a, dram):
+            for q in range(4):
+                queue.dma_start(
+                    out=w_scales[32 * q : 32 * q + 4, a * N : (a + 1) * N].bitcast(I32),
+                    in_=dram[0, 4 * q : 4 * q + 4, :].bitcast(I32),
+                )
+
+        def interleave(engine_copy, h, a, c0, c1):
+            engine_copy(
+                out=grouped[h, a][:, c0:c1, :].rearrange("p (c i) t -> p c t i", i=4),
+                in_=raw[h, a][:, :, c0:c1].rearrange("p t (c i) -> p c t i", i=4),
+            )
+
+        def quantize(h, a, c0, c1):
+            nc.vector.quantize_mx(
+                out=codes[h, a][:, c0:c1].bitcast(E5M2),
+                scales=scales[h, a][:, c0:c1],
+                in_=grouped[h, a][:, c0:c1, :].rearrange("p j t -> p (j t)"),
+            )
+
+        banks = {}
+        staged = {}
+        for h in range(2):
+            for b in range(BLOCKS):
+                banks[h, b] = psum.tile([P, HALF], F32, name="bank%d%d" % (h, b))
+
+        def multiply(h, b, order):
+            n0, n1 = b * P, (b + 1) * P
+            weights = [w8[:, n0:n1].bitcast(E4M3), w4[:, 2 * n0 : 2 * n1].bitcast(E2M1)]
+            for a in order:
+                nc.tensor.matmul_mx(
+                    out=banks[h, b][:],
+                    lhsT=weights[a],
+                    lhsT_scale=w_scales[:, a * N + n0 : a * N + n1],
+                    rhs=codes[h, a].bitcast(E5M2),
+                    rhs_scale=scales[h, a],
+                    start=(a == order[0]),
+                    stop=(a == order[1]),
+                )
+
+        def evacuate(h, b, tag):
+            staged[h, b] = keep.tile([P, HALF], F32, name="staged%d%d" % (h, b), tag=tag, align_bytes=64)
+            nc.scalar.copy(out=staged[h, b][:], in_=banks[h, b][:])
+
+        def zero_window_on(tag):
+            window = keep.tile([P, T], F32, name="window_on_" + tag, tag=tag, align_bytes=64)
+            nc.gpsimd.memset(window[:], 0.0)
+            windows.append(window)
+
+        def scatter(h, b):
+            places = offsets[:, h * LIST_COLS : (h + 1) * LIST_COLS]
+            nc.vector.tensor_tensor(windows[b % WINDOWS][:].indirect(places), staged[h, b][:], gains[h][:], MULT)
+
+        def store(b):
+            nc.sync.dma_start(out=out[b * P : (b + 1) * P, :], in_=windows[b % WINDOWS][:])
+
+        nc.gpsimd.memset(w_scales[:].bitcast(U32), 0)
+        for window in windows:
+            nc.vector.memset(window[:], 0.0)
+
+        load_dy(0, 0, 0, 256)
+        load_w8(0, P)
+        load_scales(nc.sync, 0, w8_scales)
+        load_dy(0, 0, 256, HALF)
+        load_dy(0, 1, 0, 256)
+        load_dy(0, 1, 256, HALF)
+        load_w4(0, P)
+        load_scales(nc.sync, 1, w4_scales)
+        nc.sync.dma_start(offsets[:], offs)
+        nc.sync.dma_start(out=gains[0][:], in_=wgo[:, 0:HALF])
+        load_w8(P, N)
+        load_w4(P, N)
+        load_dy(1, 0, 0, HALF)
+        load_dy(1, 1, 0, HALF)
+        nc.sync.dma_start(out=gains[1][:], in_=wgo[:, HALF:J])
+
+        interleave(nc.scalar.copy, 0, 0, 0, 256)
+        interleave(nc.vector.tensor_copy, 0, 0, 256, HALF)
+        quantize(0, 0, 0, 256)
+        quantize(0, 0, 256, HALF)
+        interleave(nc.scalar.copy, 0, 1, 0, 128)
+        interleave(nc.vector.tensor_copy, 0, 1, 128, 256)
+        quantize(0, 1, 0, 256)
+        interleave(nc.vector.tensor_copy, 0, 1, 256, 432)
+        interleave(nc.scalar.copy, 0, 1, 432, HALF)
+        quantize(0, 1, 256, HALF)
+
+        multiply(0, 0, (0, 1))
+        for b in range(1, BLOCKS):
+            multiply(0, b, (1, 0))
+        for b in range(BLOCKS - 1):
+            evacuate(0, b, "staged0%d" % b)
+        for a, tag in enumerate(("scales0", "codes0")):
+            grouped[1, a] = keep.tile([P, HALF, PACK], BF16, name="grouped1%d" % a, tag=tag, align_bytes=64)
+            interleave(nc.scalar.copy, 1, a, 0, HALF)
+        scatter(0, 0)
+        zero_window_on("staged00")
+        scatter(0, 1)
+        zero_window_on("staged01")
+        scatter(0, 2)
+        for a in range(2):
+            quantize(1, a, 0, HALF)
+        evacuate(0, 3, "scales0")
+        scatter(0, 3)
+        for b in range(BLOCKS):
+            multiply(1, b, (1, 0))
+            evacuate(1, b, "staged1%d" % b)
+        for b in range(BLOCKS):
+            scatter(1, b)
+            store(b)

@@ -35,7 +35,7 @@ def tile_list_embg_mix_none_kernel(tc, dy, w8_words, w8_scales, w4_words, w4_sca
         w_scales = keep.tile([P, 2 * N], U8, name="w_scales", align_bytes=64)
         w8 = keep.tile([P, N], U32, name="w8", align_bytes=64)
         w4 = keep.tile([P, 2 * N], U8, name="w4", align_bytes=64)
-        windows = [keep.tile([P, T], F32, name="window%d" % b) for b in range(2)]
+        windows = [keep.tile([P, T], F32, name="window%d" % b) for b in range(3)]
         gains = [keep.tile([P, HALF], F32, name="gain%d" % h) for h in range(2)]
         raw = {}
         grouped = {}
@@ -111,7 +111,7 @@ def tile_list_embg_mix_none_kernel(tc, dy, w8_words, w8_scales, w4_words, w4_sca
 
         def zero_window_on(tag):
             window = keep.tile([P, T], F32, name="window_on_" + tag, tag=tag, align_bytes=64)
-            nc.gpsimd.memset(window[:], 0.0)
+            nc.vector.memset(window[:].bitcast(I32), 0)
             windows.append(window)
 
         def scatter(h, b):
@@ -123,7 +123,7 @@ def tile_list_embg_mix_none_kernel(tc, dy, w8_words, w8_scales, w4_words, w4_sca
 
         nc.gpsimd.memset(w_scales[:].bitcast(U32), 0)
         for window in windows:
-            nc.vector.memset(window[:], 0.0)
+            nc.vector.memset(window[:].bitcast(I32), 0)
 
         load_dy(0, 0, 0, 256)
         load_w8(0, P)
@@ -152,6 +152,8 @@ def tile_list_embg_mix_none_kernel(tc, dy, w8_words, w8_scales, w4_words, w4_sca
         interleave(nc.scalar.copy, 0, 1, 432, HALF)
         quantize(0, 1, 256, HALF)
 
+        zero_window_on("grouped0")
+
         multiply(0, 0, (0, 1))
         for b in range(1, BLOCKS):
             multiply(0, b, (1, 0))
@@ -161,9 +163,7 @@ def tile_list_embg_mix_none_kernel(tc, dy, w8_words, w8_scales, w4_words, w4_sca
             grouped[1, a] = keep.tile([P, HALF, PACK], BF16, name="grouped1%d" % a, tag=tag, align_bytes=64)
             interleave(nc.scalar.copy, 1, a, 0, HALF)
         scatter(0, 0)
-        zero_window_on("staged00")
         scatter(0, 1)
-        zero_window_on("staged01")
         scatter(0, 2)
         for a in range(2):
             quantize(1, a, 0, HALF)

@@ -23,6 +23,8 @@ HALF = 512
 BLOCKS = N // P
 LIST_COLS = HALF // 16
 WINDOWS = 4
+PIECE = 256
+SHARE = 160
 
 
 def tile_list_embg_mix_none_kernel(tc, dy, w8_words, w8_scales, w4_words, w4_scales, wgo, offs, out):
@@ -35,7 +37,7 @@ def tile_list_embg_mix_none_kernel(tc, dy, w8_words, w8_scales, w4_words, w4_sca
         w_scales = keep.tile([P, 2 * N], U8, name="w_scales", align_bytes=64)
         w8 = keep.tile([P, N], U32, name="w8", align_bytes=64)
         w4 = keep.tile([P, 2 * N], U8, name="w4", align_bytes=64)
-        windows = [keep.tile([P, T], F32, name="window%d" % b) for b in range(3)]
+        windows = [keep.tile([P, T], F32, name="window%d" % b) for b in range(2)]
         gains = [keep.tile([P, HALF], F32, name="gain%d" % h) for h in range(2)]
         raw = {}
         grouped = {}
@@ -46,7 +48,7 @@ def tile_list_embg_mix_none_kernel(tc, dy, w8_words, w8_scales, w4_words, w4_sca
             codes_h = keep.tile([P, 2, HALF], U32, name="codes%d" % h, tag="codes%d" % h, align_bytes=64)
             scales_h = keep.tile([P, 2, HALF], U8, name="scales%d" % h, tag="scales%d" % h, align_bytes=64)
             for a in range(2):
-                raw[h, a] = keep.tile([P, PACK, HALF], F32, name="raw%d%d" % (h, a))
+                raw[h, a] = keep.tile([P, PACK, HALF], F32, name="raw%d%d" % (h, a), tag="raw%d%d" % (h, a), align_bytes=64)
                 codes[h, a] = codes_h[:, a]
                 scales[h, a] = scales_h[:, a]
         for a in range(2):
@@ -111,7 +113,7 @@ def tile_list_embg_mix_none_kernel(tc, dy, w8_words, w8_scales, w4_words, w4_sca
 
         def zero_window_on(tag):
             window = keep.tile([P, T], F32, name="window_on_" + tag, tag=tag, align_bytes=64)
-            nc.vector.memset(window[:].bitcast(I32), 0)
+            nc.gpsimd.memset(window[:].bitcast(I32), 0)
             windows.append(window)
 
         def scatter(h, b):
@@ -121,53 +123,52 @@ def tile_list_embg_mix_none_kernel(tc, dy, w8_words, w8_scales, w4_words, w4_sca
         def store(b):
             nc.sync.dma_start(out=out[b * P : (b + 1) * P, :], in_=windows[b % WINDOWS][:])
 
-        nc.gpsimd.memset(w_scales[:].bitcast(U32), 0)
         for window in windows:
             nc.vector.memset(window[:].bitcast(I32), 0)
 
         load_dy(0, 0, 0, 256)
-        load_w8(0, P)
         load_scales(nc.sync, 0, w8_scales)
         load_dy(0, 0, 256, HALF)
         load_dy(0, 1, 0, 256)
         load_dy(0, 1, 256, HALF)
-        load_w4(0, P)
+        load_w8(0, P)
         load_scales(nc.sync, 1, w4_scales)
-        nc.sync.dma_start(offsets[:], offs)
+        load_w4(0, P)
         nc.sync.dma_start(out=gains[0][:], in_=wgo[:, 0:HALF])
+        nc.sync.dma_start(offsets[:], offs)
         load_w8(P, N)
         load_w4(P, N)
         load_dy(1, 0, 0, HALF)
         load_dy(1, 1, 0, HALF)
         nc.sync.dma_start(out=gains[1][:], in_=wgo[:, HALF:J])
 
-        interleave(nc.scalar.copy, 0, 0, 0, 256)
-        interleave(nc.vector.tensor_copy, 0, 0, 256, HALF)
-        quantize(0, 0, 0, 256)
-        quantize(0, 0, 256, HALF)
-        interleave(nc.scalar.copy, 0, 1, 0, 128)
-        interleave(nc.vector.tensor_copy, 0, 1, 128, 256)
-        quantize(0, 1, 0, 256)
-        interleave(nc.vector.tensor_copy, 0, 1, 256, 432)
-        interleave(nc.scalar.copy, 0, 1, 432, HALF)
-        quantize(0, 1, 256, HALF)
-
-        zero_window_on("grouped0")
+        for a in range(2):
+            for c0 in range(0, HALF, PIECE):
+                interleave(nc.vector.tensor_copy, 0, a, c0, c0 + SHARE)
+                interleave(nc.scalar.copy, 0, a, c0 + SHARE, c0 + PIECE)
+                quantize(0, a, c0, c0 + PIECE)
 
         multiply(0, 0, (0, 1))
         for b in range(1, BLOCKS):
             multiply(0, b, (1, 0))
-        for b in range(BLOCKS - 1):
+        first = keep.tile([P, P], F32, name="first", align_bytes=64)
+        second = keep.tile([P, HALF - P], F32, name="second", align_bytes=64)
+        nc.vector.tensor_copy(out=first[:], in_=banks[0, 0][:, 0:P])
+        nc.scalar.copy(out=second[:], in_=banks[0, 0][:, P:HALF])
+        nc.vector.tensor_tensor(windows[0][:].indirect(offsets[:, 0 : P // 16]), first[:], gains[0][:, 0:P], MULT)
+        nc.vector.tensor_tensor(windows[0][:].indirect(offsets[:, P // 16 : LIST_COLS]), second[:], gains[0][:, P:HALF], MULT)
+        zero_window_on("first")
+        zero_window_on("second")
+        for b in range(1, BLOCKS - 1):
             evacuate(0, b, "staged0%d" % b)
         for a, tag in enumerate(("scales0", "codes0")):
             grouped[1, a] = keep.tile([P, HALF, PACK], BF16, name="grouped1%d" % a, tag=tag, align_bytes=64)
             interleave(nc.scalar.copy, 1, a, 0, HALF)
-        scatter(0, 0)
         scatter(0, 1)
         scatter(0, 2)
         for a in range(2):
             quantize(1, a, 0, HALF)
-        evacuate(0, 3, "scales0")
+        evacuate(0, 3, "raw11")
         scatter(0, 3)
         for b in range(BLOCKS):
             multiply(1, b, (1, 0))

@@ -21,10 +21,9 @@ PACK = 4
 K_PASS = P * PACK
 HALF = 512
 BLOCKS = N // P
-LIST_COLS = HALF // 16
-WINDOWS = 4
 PIECE = 256
 SHARE = 160
+LEAD = 128
 
 
 def tile_list_embg_mix_none_kernel(tc, dy, w8_words, w8_scales, w4_words, w4_scales, wgo, offs, out):
@@ -38,28 +37,23 @@ def tile_list_embg_mix_none_kernel(tc, dy, w8_words, w8_scales, w4_words, w4_sca
         w8 = keep.tile([P, N], U32, name="w8", align_bytes=64)
         w4 = keep.tile([P, 2 * N], U8, name="w4", align_bytes=64)
         windows = [keep.tile([P, T], F32, name="window%d" % b) for b in range(2)]
-        gains = [keep.tile([P, HALF], F32, name="gain%d" % h) for h in range(2)]
-        raw = {}
-        grouped = {}
+        gains = keep.tile([P, J], F32, name="gains")
         codes = {}
         scales = {}
-        grouped_0 = keep.tile([P, 2, HALF, PACK], BF16, name="grouped0", tag="grouped0", align_bytes=64)
         for h in range(2):
-            codes_h = keep.tile([P, 2, HALF], U32, name="codes%d" % h, tag="codes%d" % h, align_bytes=64)
-            scales_h = keep.tile([P, 2, HALF], U8, name="scales%d" % h, tag="scales%d" % h, align_bytes=64)
             for a in range(2):
-                raw[h, a] = keep.tile([P, PACK, HALF], F32, name="raw%d%d" % (h, a), tag="raw%d%d" % (h, a), align_bytes=64)
-                codes[h, a] = codes_h[:, a]
-                scales[h, a] = scales_h[:, a]
-        for a in range(2):
-            grouped[0, a] = grouped_0[:, a]
+                codes[h, a] = keep.tile([P, HALF], U32, name="codes%d%d" % (h, a), tag="codes%d%d" % (h, a), align_bytes=64)
+                scales[h, a] = keep.tile([P, HALF], U8, name="scales%d%d" % (h, a), tag="scales%d%d" % (h, a), align_bytes=64)
 
         w8_dram = w8_words[0].rearrange("p n t -> p (n t)").bitcast(I32)
         w4_dram = w4_words[0].bitcast(I32)
+        raw = {}
+        grouped = {}
 
-        def load_dy(h, a, c0, c1):
-            rows = dy[a * K_PASS : (a + 1) * K_PASS, h * HALF + c0 : h * HALF + c1]
-            nc.sync.dma_start(out=raw[h, a][:, :, c0:c1], in_=rows.rearrange("(p t) j -> p t j", t=PACK))
+        def load_dy(a, j0, j1):
+            raw[a, j0] = keep.tile([P, PACK, j1 - j0], F32, name="raw%d_%d" % (a, j0), tag="raw%d_%d" % (a, j0), align_bytes=64)
+            rows = dy[a * K_PASS : (a + 1) * K_PASS, j0:j1]
+            nc.sync.dma_start(out=raw[a, j0][:], in_=rows.rearrange("(p t) j -> p t j", t=PACK))
 
         def load_w8(n0, n1):
             nc.sync.dma_start(out=w8[:, n0:n1].bitcast(I32), in_=w8_dram[:, n0:n1])
@@ -67,112 +61,127 @@ def tile_list_embg_mix_none_kernel(tc, dy, w8_words, w8_scales, w4_words, w4_sca
         def load_w4(n0, n1):
             nc.sync.dma_start(out=w4[:, 2 * n0 : 2 * n1].bitcast(I32), in_=w4_dram[:, n0 // 2 : n1 // 2])
 
-        def load_scales(queue, a, dram):
-            for q in range(4):
-                queue.dma_start(
-                    out=w_scales[32 * q : 32 * q + 4, a * N : (a + 1) * N].bitcast(I32),
-                    in_=dram[0, 4 * q : 4 * q + 4, :].bitcast(I32),
-                )
+        def load_scales(a, dram, q):
+            nc.sync.dma_start(
+                out=w_scales[32 * q : 32 * q + 4, a * N : (a + 1) * N].bitcast(I32),
+                in_=dram[0, 4 * q : 4 * q + 4, :].bitcast(I32),
+            )
 
-        def interleave(engine_copy, h, a, c0, c1):
+        def load_gains(j0, j1):
+            nc.sync.dma_start(out=gains[:, j0:j1], in_=wgo[:, j0:j1])
+
+        def new_grouped(a, j0, width, tag):
+            grouped[a, j0] = keep.tile([P, width, PACK], BF16, name="grouped%d_%d" % (a, j0), tag=tag, align_bytes=64)
+
+        def interleave(engine_copy, a, j0, c0, c1):
             engine_copy(
-                out=grouped[h, a][:, c0:c1, :].rearrange("p (c i) t -> p c t i", i=4),
-                in_=raw[h, a][:, :, c0:c1].rearrange("p t (c i) -> p c t i", i=4),
+                out=grouped[a, j0][:, c0:c1, :].rearrange("p (c i) t -> p c t i", i=4),
+                in_=raw[a, j0][:, :, c0:c1].rearrange("p t (c i) -> p c t i", i=4),
             )
 
-        def quantize(h, a, c0, c1):
+        def quantize(a, j0, width):
+            h, c0 = divmod(j0, HALF)
             nc.vector.quantize_mx(
-                out=codes[h, a][:, c0:c1].bitcast(E5M2),
-                scales=scales[h, a][:, c0:c1],
-                in_=grouped[h, a][:, c0:c1, :].rearrange("p j t -> p (j t)"),
+                out=codes[h, a][:, c0 : c0 + width].bitcast(E5M2),
+                scales=scales[h, a][:, c0 : c0 + width],
+                in_=grouped[a, j0][:].rearrange("p j t -> p (j t)"),
             )
 
-        banks = {}
-        staged = {}
-        for h in range(2):
-            for b in range(BLOCKS):
-                banks[h, b] = psum.tile([P, HALF], F32, name="bank%d%d" % (h, b))
+        def new_bank(name, tag):
+            return psum.tile([P, HALF], F32, name=name, tag=tag)
 
-        def multiply(h, b, order):
+        def one_pass(bank, h, b, a, start, stop):
             n0, n1 = b * P, (b + 1) * P
             weights = [w8[:, n0:n1].bitcast(E4M3), w4[:, 2 * n0 : 2 * n1].bitcast(E2M1)]
-            for a in order:
-                nc.tensor.matmul_mx(
-                    out=banks[h, b][:],
-                    lhsT=weights[a],
-                    lhsT_scale=w_scales[:, a * N + n0 : a * N + n1],
-                    rhs=codes[h, a].bitcast(E5M2),
-                    rhs_scale=scales[h, a],
-                    start=(a == order[0]),
-                    stop=(a == order[1]),
-                )
+            nc.tensor.matmul_mx(
+                out=bank[:],
+                lhsT=weights[a],
+                lhsT_scale=w_scales[:, a * N + n0 : a * N + n1],
+                rhs=codes[h, a][:].bitcast(E5M2),
+                rhs_scale=scales[h, a][:],
+                start=start,
+                stop=stop,
+            )
 
-        def evacuate(h, b, tag):
-            staged[h, b] = keep.tile([P, HALF], F32, name="staged%d%d" % (h, b), tag=tag, align_bytes=64)
-            nc.scalar.copy(out=staged[h, b][:], in_=banks[h, b][:])
+        def multiply(h, b, order):
+            bank = new_bank("bank%d%d" % (h, b), "bank%d%d" % (h, b))
+            one_pass(bank, h, b, order[0], True, False)
+            one_pass(bank, h, b, order[1], False, True)
+            return bank
+
+        def new_staged(name, width, tag):
+            return keep.tile([P, width], F32, name=name, tag=tag, align_bytes=64)
 
         def zero_window_on(tag):
             window = keep.tile([P, T], F32, name="window_on_" + tag, tag=tag, align_bytes=64)
             nc.gpsimd.memset(window[:].bitcast(I32), 0)
             windows.append(window)
 
-        def scatter(h, b):
-            places = offsets[:, h * LIST_COLS : (h + 1) * LIST_COLS]
-            nc.vector.tensor_tensor(windows[b % WINDOWS][:].indirect(places), staged[h, b][:], gains[h][:], MULT)
+        def scatter(b, values, j0, j1):
+            nc.vector.tensor_tensor(windows[b][:].indirect(offsets[:, j0 // 16 : j1 // 16]), values, gains[:, j0:j1], MULT)
 
         def store(b):
-            nc.sync.dma_start(out=out[b * P : (b + 1) * P, :], in_=windows[b % WINDOWS][:])
+            nc.sync.dma_start(out=out[b * P : (b + 1) * P, :], in_=windows[b][:])
 
         for window in windows:
             nc.vector.memset(window[:].bitcast(I32), 0)
 
-        load_dy(0, 0, 0, 256)
-        load_scales(nc.sync, 0, w8_scales)
-        load_dy(0, 0, 256, HALF)
-        load_dy(0, 1, 0, 256)
-        load_dy(0, 1, 256, HALF)
-        load_w8(0, P)
-        load_scales(nc.sync, 1, w4_scales)
-        load_w4(0, P)
-        nc.sync.dma_start(out=gains[0][:], in_=wgo[:, 0:HALF])
+        load_dy(0, 0, HALF)
+        for q in range(4):
+            load_scales(0, w8_scales, q)
+        load_w8(0, 2 * P)
+        load_dy(1, 0, PIECE)
+        load_dy(1, PIECE, HALF)
+        for q in range(4):
+            load_scales(1, w4_scales, q)
+        load_w4(0, N)
         nc.sync.dma_start(offsets[:], offs)
-        load_w8(P, N)
-        load_w4(P, N)
-        load_dy(1, 0, 0, HALF)
-        load_dy(1, 1, 0, HALF)
-        nc.sync.dma_start(out=gains[1][:], in_=wgo[:, HALF:J])
+        load_gains(0, HALF)
+        load_w8(2 * P, N)
+        load_dy(0, HALF, J)
+        load_dy(1, HALF, J)
+        load_gains(HALF, J)
 
+        for a, j0, width in ((0, 0, HALF), (1, 0, PIECE), (1, PIECE, PIECE)):
+            share = SHARE * width // PIECE
+            new_grouped(a, j0, width, "grouped%d_%d" % (a, j0))
+            interleave(nc.vector.tensor_copy, a, j0, 0, share)
+            interleave(nc.scalar.copy, a, j0, share, width)
+            quantize(a, j0, width)
+
+        banks = {b: new_bank("bank0%d" % b, "bank0%d" % b) for b in range(2)}
         for a in range(2):
-            for c0 in range(0, HALF, PIECE):
-                interleave(nc.vector.tensor_copy, 0, a, c0, c0 + SHARE)
-                interleave(nc.scalar.copy, 0, a, c0 + SHARE, c0 + PIECE)
-                quantize(0, a, c0, c0 + PIECE)
+            for b in range(2):
+                one_pass(banks[b], 0, b, a, a == 0, a == 1)
+        for b in range(2, BLOCKS):
+            banks[b] = multiply(0, b, (1, 0))
 
-        multiply(0, 0, (0, 1))
-        for b in range(1, BLOCKS):
-            multiply(0, b, (1, 0))
-        first = keep.tile([P, P], F32, name="first", align_bytes=64)
-        second = keep.tile([P, HALF - P], F32, name="second", align_bytes=64)
-        nc.vector.tensor_copy(out=first[:], in_=banks[0, 0][:, 0:P])
-        nc.scalar.copy(out=second[:], in_=banks[0, 0][:, P:HALF])
-        nc.vector.tensor_tensor(windows[0][:].indirect(offsets[:, 0 : P // 16]), first[:], gains[0][:, 0:P], MULT)
-        nc.vector.tensor_tensor(windows[0][:].indirect(offsets[:, P // 16 : LIST_COLS]), second[:], gains[0][:, P:HALF], MULT)
+        def evacuate(bank, name, tag):
+            staged = new_staged(name, HALF, tag)
+            nc.scalar.copy(out=staged[:], in_=bank[:])
+            return staged
+
+        first = new_staged("first", LEAD, "first")
+        nc.vector.tensor_copy(out=first[:], in_=banks[0][:, 0:LEAD])
+        scatter(0, first[:], 0, LEAD)
+        staged1 = evacuate(banks[1], "staged01", "staged01")
+        second = new_staged("second", HALF - LEAD, "second")
+        nc.scalar.copy(out=second[:], in_=banks[0][:, LEAD:HALF])
+        staged2 = evacuate(banks[2], "staged02", "staged02")
         zero_window_on("first")
-        zero_window_on("second")
-        for b in range(1, BLOCKS - 1):
-            evacuate(0, b, "staged0%d" % b)
-        for a, tag in enumerate(("scales0", "codes0")):
-            grouped[1, a] = keep.tile([P, HALF, PACK], BF16, name="grouped1%d" % a, tag=tag, align_bytes=64)
-            interleave(nc.scalar.copy, 1, a, 0, HALF)
-        scatter(0, 1)
-        scatter(0, 2)
+        scatter(1, staged1[:], 0, HALF)
+        zero_window_on("staged01")
+        scatter(0, second[:], LEAD, HALF)
+        for a, tag in enumerate(("scales01", "codes01")):
+            new_grouped(a, HALF, HALF, tag)
+            interleave(nc.scalar.copy, a, HALF, 0, HALF)
+        scatter(2, staged2[:], 0, HALF)
         for a in range(2):
-            quantize(1, a, 0, HALF)
-        evacuate(0, 3, "raw11")
-        scatter(0, 3)
+            quantize(a, HALF, HALF)
+        staged3 = evacuate(banks[3], "staged03", "raw1_512")
+        scatter(3, staged3[:], 0, HALF)
+
+        later = [evacuate(multiply(1, b, (1, 0)), "staged1%d" % b, "staged1%d" % b) for b in range(BLOCKS)]
         for b in range(BLOCKS):
-            multiply(1, b, (1, 0))
-            evacuate(1, b, "staged1%d" % b)
-        for b in range(BLOCKS):
-            scatter(1, b)
+            scatter(b, later[b][:], HALF, J)
             store(b)

@@ -1,6 +1,7 @@
 from contextlib import ExitStack
 
 import concourse.mybir as mybir
+from concourse.masks import make_identity
 
 K, N, T, J = 1024, 512, 2048, 1024
 FLOPS = 2 * K * N * J
@@ -21,9 +22,8 @@ PACK = 4
 K_PASS = P * PACK
 HALF = 512
 BLOCKS = N // P
+CHUNK = 128
 PIECE = 256
-SHARE = 160
-LEAD = 128
 
 
 def tile_list_embg_mix_none_kernel(tc, dy, w8_words, w8_scales, w4_words, w4_scales, wgo, offs, out):
@@ -32,156 +32,206 @@ def tile_list_embg_mix_none_kernel(tc, dy, w8_words, w8_scales, w4_words, w4_sca
         keep = ctx.enter_context(tc.tile_pool(name="keep", bufs=1))
         psum = ctx.enter_context(tc.psum_pool(name="psum", bufs=1))
 
-        offsets = keep.tile([P, J // 16], U16, name="offsets")
-        w_scales = keep.tile([P, 2 * N], U8, name="w_scales", align_bytes=64)
-        w8 = keep.tile([P, N], U32, name="w8", align_bytes=64)
-        w4 = keep.tile([P, 2 * N], U8, name="w4", align_bytes=64)
-        windows = [keep.tile([P, T], F32, name="window%d" % b) for b in range(2)]
-        gains = keep.tile([P, J], F32, name="gains")
-        codes = {}
-        scales = {}
-        for h in range(2):
-            for a in range(2):
-                codes[h, a] = keep.tile([P, HALF], U32, name="codes%d%d" % (h, a), tag="codes%d%d" % (h, a), align_bytes=64)
-                scales[h, a] = keep.tile([P, HALF], U8, name="scales%d%d" % (h, a), tag="scales%d%d" % (h, a), align_bytes=64)
+        def sbuf(shape, dtype, name, tag=None):
+            return keep.tile(shape, dtype, name=name, tag=tag or name, align_bytes=64)
 
-        w8_dram = w8_words[0].rearrange("p n t -> p (n t)").bitcast(I32)
-        w4_dram = w4_words[0].bitcast(I32)
+        offsets = keep.tile([P, J // 16], U16, name="offsets")
+        w_scales = sbuf([P, 2 * N], U8, "w_scales")
+        w8 = sbuf([P, N], U32, "w8")
+        w4 = sbuf([P, 2 * N], U8, "w4")
+        windows = [sbuf([P, T], F32, "window%d" % b) for b in range(3)]
+        gains = sbuf([P, J], F32, "gains")
+        identity = sbuf([P, P], F32, "identity")
+
         raw = {}
-        grouped = {}
 
         def load_dy(a, j0, j1):
-            raw[a, j0] = keep.tile([P, PACK, j1 - j0], F32, name="raw%d_%d" % (a, j0), tag="raw%d_%d" % (a, j0), align_bytes=64)
+            tile = sbuf([P, PACK, j1 - j0], F32, "raw%d_%d" % (a, j0))
             rows = dy[a * K_PASS : (a + 1) * K_PASS, j0:j1]
-            nc.sync.dma_start(out=raw[a, j0][:], in_=rows.rearrange("(p t) j -> p t j", t=PACK))
+            nc.sync.dma_start(out=tile[:], in_=rows.rearrange("(p t) j -> p t j", t=PACK))
+            for j in range(j0, j1, CHUNK):
+                raw[a, j] = (tile, j - j0)
 
-        def load_w8(n0, n1):
-            nc.sync.dma_start(out=w8[:, n0:n1].bitcast(I32), in_=w8_dram[:, n0:n1])
-
-        def load_w4(n0, n1):
-            nc.sync.dma_start(out=w4[:, 2 * n0 : 2 * n1].bitcast(I32), in_=w4_dram[:, n0 // 2 : n1 // 2])
-
-        def load_scales(a, dram, q):
-            nc.sync.dma_start(
-                out=w_scales[32 * q : 32 * q + 4, a * N : (a + 1) * N].bitcast(I32),
-                in_=dram[0, 4 * q : 4 * q + 4, :].bitcast(I32),
-            )
+        def load_scales(a, dram):
+            for q in range(4):
+                nc.sync.dma_start(
+                    out=w_scales[32 * q : 32 * q + 4, a * N : (a + 1) * N].bitcast(I32),
+                    in_=dram[0, 4 * q : 4 * q + 4, :].bitcast(I32),
+                )
 
         def load_gains(j0, j1):
             nc.sync.dma_start(out=gains[:, j0:j1], in_=wgo[:, j0:j1])
 
-        def new_grouped(a, j0, width, tag):
-            grouped[a, j0] = keep.tile([P, width, PACK], BF16, name="grouped%d_%d" % (a, j0), tag=tag, align_bytes=64)
-
-        def interleave(engine_copy, a, j0, c0, c1):
+        def interleave(engine_copy, grouped, a, j0, width):
+            tile, c0 = raw[a, j0]
             engine_copy(
-                out=grouped[a, j0][:, c0:c1, :].rearrange("p (c i) t -> p c t i", i=4),
-                in_=raw[a, j0][:, :, c0:c1].rearrange("p t (c i) -> p c t i", i=4),
+                out=grouped.rearrange("p (c i) t -> p c t i", i=4),
+                in_=tile[:, :, c0 : c0 + width].rearrange("p t (c i) -> p c t i", i=4),
             )
 
-        def quantize(a, j0, width):
-            h, c0 = divmod(j0, HALF)
-            nc.vector.quantize_mx(
-                out=codes[h, a][:, c0 : c0 + width].bitcast(E5M2),
-                scales=scales[h, a][:, c0 : c0 + width],
-                in_=grouped[a, j0][:].rearrange("p j t -> p (j t)"),
-            )
-
-        def new_bank(name, tag):
-            return psum.tile([P, HALF], F32, name=name, tag=tag)
-
-        def one_pass(bank, h, b, a, start, stop):
-            n0, n1 = b * P, (b + 1) * P
-            weights = [w8[:, n0:n1].bitcast(E4M3), w4[:, 2 * n0 : 2 * n1].bitcast(E2M1)]
-            nc.tensor.matmul_mx(
-                out=bank[:],
-                lhsT=weights[a],
-                lhsT_scale=w_scales[:, a * N + n0 : a * N + n1],
-                rhs=codes[h, a][:].bitcast(E5M2),
-                rhs_scale=scales[h, a][:],
-                start=start,
-                stop=stop,
-            )
-
-        def multiply(h, b, order):
-            bank = new_bank("bank%d%d" % (h, b), "bank%d%d" % (h, b))
-            one_pass(bank, h, b, order[0], True, False)
-            one_pass(bank, h, b, order[1], False, True)
-            return bank
-
-        def new_staged(name, width, tag):
-            return keep.tile([P, width], F32, name=name, tag=tag, align_bytes=64)
-
-        def zero_window_on(tag):
-            window = keep.tile([P, T], F32, name="window_on_" + tag, tag=tag, align_bytes=64)
-            nc.gpsimd.memset(window[:].bitcast(I32), 0)
-            windows.append(window)
+        def quantize(codes, scales, grouped):
+            nc.vector.quantize_mx(out=codes.bitcast(E5M2), scales=scales, in_=grouped)
 
         def scatter(b, values, j0, j1):
             nc.vector.tensor_tensor(windows[b][:].indirect(offsets[:, j0 // 16 : j1 // 16]), values, gains[:, j0:j1], MULT)
 
-        def store(b):
-            nc.sync.dma_start(out=out[b * P : (b + 1) * P, :], in_=windows[b][:])
+        make_identity(nc, identity[:])
+        for c0, c1 in ((0, 1023), (1023, T)):
+            nc.vector.memset(windows[0][:, c0:c1].bitcast(I32), 0)
+        nc.gpsimd.memset(windows[1][:].bitcast(I32), 0)
+        for c0, c1 in ((0, 511), (511, 1024)):
+            nc.vector.memset(windows[2][:, c0:c1].bitcast(I32), 0)
+        nc.gpsimd.memset(windows[2][:, 1024:T].bitcast(I32), 0)
 
-        for window in windows:
-            nc.vector.memset(window[:].bitcast(I32), 0)
-
-        load_dy(0, 0, HALF)
-        for q in range(4):
-            load_scales(0, w8_scales, q)
-        load_w8(0, 2 * P)
-        load_dy(1, 0, PIECE)
-        load_dy(1, PIECE, HALF)
-        for q in range(4):
-            load_scales(1, w4_scales, q)
-        load_w4(0, N)
+        load_dy(0, 0, CHUNK)
+        load_scales(0, w8_scales)
+        load_dy(1, 0, CHUNK)
+        nc.sync.dma_start(out=w8[:].bitcast(I32), in_=w8_words[0].rearrange("p n t -> p (n t)").bitcast(I32))
+        nc.sync.dma_start(out=w4[:].bitcast(I32), in_=w4_words[0].bitcast(I32))
+        load_scales(1, w4_scales)
+        load_dy(0, CHUNK, 2 * CHUNK)
+        load_dy(1, CHUNK, 2 * CHUNK)
         nc.sync.dma_start(offsets[:], offs)
-        load_gains(0, HALF)
-        load_w8(2 * P, N)
-        load_dy(0, HALF, J)
-        load_dy(1, HALF, J)
+        load_gains(0, 2 * CHUNK)
+        for c in (2, 3):
+            load_dy(0, c * CHUNK, (c + 1) * CHUNK)
+            load_dy(1, c * CHUNK, (c + 1) * CHUNK)
+        load_dy(0, HALF, HALF + PIECE)
+        load_gains(2 * CHUNK, HALF)
+        load_dy(0, HALF + PIECE, J)
+        load_dy(1, HALF, HALF + PIECE)
+        load_dy(1, HALF + PIECE, J)
         load_gains(HALF, J)
 
-        for a, j0, width in ((0, 0, HALF), (1, 0, PIECE), (1, PIECE, PIECE)):
-            share = SHARE * width // PIECE
-            new_grouped(a, j0, width, "grouped%d_%d" % (a, j0))
-            interleave(nc.vector.tensor_copy, a, j0, 0, share)
-            interleave(nc.scalar.copy, a, j0, share, width)
-            quantize(a, j0, width)
+        def flat(grouped):
+            return grouped.rearrange("p a j t -> p (a j t)")
 
-        banks = {b: new_bank("bank0%d" % b, "bank0%d" % b) for b in range(2)}
+        def multiply_chunk(c, codes, scales, order):
+            bank = psum.tile([P, N], F32, name="tokens%d" % c, tag="tokens")
+            moving = [w8[:].bitcast(E4M3), w4[:].bitcast(E2M1)]
+            for a in range(2):
+                cols = slice(order[a] * CHUNK, (order[a] + 1) * CHUNK)
+                nc.tensor.matmul_mx(
+                    out=bank[:],
+                    lhsT=codes[:, cols].bitcast(E5M2),
+                    lhsT_scale=scales[:, cols],
+                    rhs=moving[a],
+                    rhs_scale=w_scales[:, a * N : (a + 1) * N],
+                    start=a == 0,
+                    stop=a == 1,
+                )
+            return bank
+
+        def by_block(bank, b0, b1):
+            return bank[:, b0 * P : b1 * P].rearrange("p (b c) -> p b c", c=P)
+
+        def new_codes(name, width, tag=None):
+            return sbuf([P, width], U32, "codes" + name, tag), sbuf([P, width], U8, "scales" + name)
+
+        grouped0 = sbuf([P, 2, CHUNK, PACK], BF16, "grouped0")
+        grouped1 = sbuf([P, 2, CHUNK, PACK], BF16, "grouped1")
+        codes0, scales0 = new_codes("0", 2 * CHUNK)
+        codes1, scales1 = new_codes("1", 2 * CHUNK)
         for a in range(2):
-            for b in range(2):
-                one_pass(banks[b], 0, b, a, a == 0, a == 1)
-        for b in range(2, BLOCKS):
-            banks[b] = multiply(0, b, (1, 0))
+            cols = slice(a * CHUNK, (a + 1) * CHUNK)
+            interleave(nc.vector.tensor_copy, grouped0[:, a], a, 0, CHUNK)
+            quantize(codes0[:, cols], scales0[:, cols], flat(grouped0[:, a : a + 1]))
+        def f32_blocks(name, count, tag=None):
+            return sbuf([P, count, P], F32, name, tag)
 
-        def evacuate(bank, name, tag):
-            staged = new_staged(name, HALF, tag)
-            nc.scalar.copy(out=staged[:], in_=bank[:])
-            return staged
+        def stage(bank, b0, b1, tile, slot):
+            nc.scalar.copy(out=tile[:, slot : slot + b1 - b0, :], in_=by_block(bank, b0, b1))
+            return [tile[:, slot + i, :] for i in range(b1 - b0)]
 
-        first = new_staged("first", LEAD, "first")
-        nc.vector.tensor_copy(out=first[:], in_=banks[0][:, 0:LEAD])
-        scatter(0, first[:], 0, LEAD)
-        staged1 = evacuate(banks[1], "staged01", "staged01")
-        second = new_staged("second", HALF - LEAD, "second")
-        nc.scalar.copy(out=second[:], in_=banks[0][:, LEAD:HALF])
-        staged2 = evacuate(banks[2], "staged02", "staged02")
-        zero_window_on("first")
-        scatter(1, staged1[:], 0, HALF)
-        zero_window_on("staged01")
-        scatter(0, second[:], LEAD, HALF)
-        for a, tag in enumerate(("scales01", "codes01")):
-            new_grouped(a, HALF, HALF, tag)
-            interleave(nc.scalar.copy, a, HALF, 0, HALF)
-        scatter(2, staged2[:], 0, HALF)
-        for a in range(2):
-            quantize(a, HALF, HALF)
-        staged3 = evacuate(banks[3], "staged03", "raw1_512")
-        scatter(3, staged3[:], 0, HALF)
+        def turn_back(name, rows, b0, tag):
+            back = psum.tile([P, N], F32, name=name, tag=tag)
+            for i, block in enumerate(rows):
+                nc.tensor.transpose(back[:, (b0 + i) * P : (b0 + i + 1) * P], block, identity[:])
+            return back
 
-        later = [evacuate(multiply(1, b, (1, 0)), "staged1%d" % b, "staged1%d" % b) for b in range(BLOCKS)]
+        def scatter_blocks(c, values, b0):
+            for i, block in enumerate(values):
+                scatter(b0 + i, block, c * CHUNK, (c + 1) * CHUNK)
+
+        def round_on_scalar(name, tag, pieces, width):
+            tile = sbuf([P, len(pieces), width, PACK], BF16, name, tag)
+            for i, (a, j0) in enumerate(pieces):
+                interleave(nc.scalar.copy, tile[:, i], a, j0, width)
+            return tile
+
+        bank = multiply_chunk(0, codes0, scales0, (0, 1))
+        rows0 = f32_blocks("rows0", 4)
+        lead = stage(bank, 0, 1, rows0, 0)
+        others = stage(bank, 1, 4, rows0, 1)
+        first = turn_back("first0", lead, 0, "first")
+        back0 = turn_back("back0", others, 1, "back0")
+        values00 = stage(first, 0, 1, f32_blocks("values00", 1), 0)
+        values01 = stage(back0, 1, 4, f32_blocks("values01", 3), 0)
+
+        interleave(nc.vector.tensor_copy, grouped1[:, 0], 0, CHUNK, CHUNK)
+        quantize(codes1[:, 0:CHUNK], scales1[:, 0:CHUNK], flat(grouped1[:, 0:1]))
+        interleave(nc.vector.tensor_copy, grouped1[:, 1], 1, CHUNK, CHUNK)
+        quantize(codes1[:, CHUNK:], scales1[:, CHUNK:], flat(grouped1[:, 1:2]))
+        window = sbuf([P, T], F32, "window3", "grouped1")
+        nc.gpsimd.memset(window[:].bitcast(I32), 0)
+        windows.append(window)
+        scatter_blocks(0, values00, 0)
+        scatter_blocks(0, values01, 1)
+
+        rows1 = stage(multiply_chunk(1, codes1, scales1, (0, 1)), 0, 4, f32_blocks("rows1", 4), 0)
+        back1 = turn_back("back1", rows1, 0, "back1")
+        grouped2 = round_on_scalar("grouped2", None, ((0, 2 * CHUNK), (1, 2 * CHUNK)), CHUNK)
+        values10 = stage(back1, 0, 2, f32_blocks("values10", 2, "raw1_256"), 0)
+        codes2, scales2 = new_codes("2", 2 * CHUNK, "values01")
+        quantize(codes2[:], scales2[:], flat(grouped2[:]))
+        scatter_blocks(1, values10, 0)
+
+        grouped3 = round_on_scalar("grouped3", None, ((0, 3 * CHUNK), (1, 3 * CHUNK)), CHUNK)
+        low4 = round_on_scalar("low4", "grouped2", ((0, HALF),), PIECE)
+        after4 = f32_blocks("after4", 6, "raw0_512")
+        values12 = stage(back1, 2, 4, after4, 0)
+        rows2 = stage(multiply_chunk(2, codes2, scales2, (0, 1)), 0, 4, after4, 2)
+        codes3, scales3 = new_codes("3", 2 * CHUNK, "raw1_256")
+        quantize(codes3[:], scales3[:], flat(grouped3[:]))
+        low_codes, low_scales = new_codes("low", HALF)
+        quantize(low_codes[:, 0:PIECE], low_scales[:, 0:PIECE], flat(low4[:]))
+        scatter_blocks(1, values12, 2)
+
+        back2 = turn_back("back2", rows2, 0, "back0")
+        low5 = round_on_scalar("low5", "grouped2", ((0, HALF + PIECE),), PIECE)
+        values2 = f32_blocks("values2", 4)
+        values20 = stage(back2, 0, 1, values2, 0)
+        values21 = stage(back2, 1, 4, values2, 1)
+        quantize(low_codes[:, PIECE:], low_scales[:, PIECE:], flat(low5[:]))
+        scatter_blocks(2, values20 + values21, 0)
+
+        rows3 = stage(multiply_chunk(3, codes3, scales3, (0, 1)), 0, 4, f32_blocks("rows3", 4), 0)
+        back3 = turn_back("back3", rows3, 0, "back1")
+        high = round_on_scalar("high", "raw1_256", ((1, HALF), (1, HALF + PIECE)), PIECE)
+        values3 = f32_blocks("values3", 4, "raw1_768")
+        values30 = stage(back3, 0, 1, values3, 0)
+        values31 = stage(back3, 1, 4, values3, 1)
+        high_codes, high_scales = new_codes("high", HALF, "values2")
+        quantize(high_codes[:], high_scales[:], flat(high[:]))
+        scatter_blocks(3, values30 + values31, 0)
+
+        late_codes = [low_codes, high_codes]
+        late_scales = [low_scales, high_scales]
         for b in range(BLOCKS):
-            scatter(b, later[b][:], HALF, J)
-            store(b)
+            n0, n1 = b * P, (b + 1) * P
+            bank = psum.tile([P, HALF], F32, name="late%d" % b, tag="late%d" % b)
+            weights = [w8[:, n0:n1].bitcast(E4M3), w4[:, 2 * n0 : 2 * n1].bitcast(E2M1)]
+            for a in range(2):
+                nc.tensor.matmul_mx(
+                    out=bank[:],
+                    lhsT=weights[a],
+                    lhsT_scale=w_scales[:, a * N + n0 : a * N + n1],
+                    rhs=late_codes[a][:].bitcast(E5M2),
+                    rhs_scale=late_scales[a][:],
+                    start=a == 0,
+                    stop=a == 1,
+                )
+            staged = sbuf([P, HALF], F32, "late_staged%d" % b)
+            nc.scalar.copy(out=staged[:], in_=bank[:])
+            scatter(b, staged[:], HALF, J)
+            nc.sync.dma_start(out=out[n0:n1, :], in_=windows[b][:])

@@ -39,7 +39,7 @@ def tile_list_embg_mix_none_kernel(tc, dy, w8_words, w8_scales, w4_words, w4_sca
         w_scales = sbuf([P, 2 * N], U8, "w_scales")
         w8 = sbuf([P, N], U32, "w8")
         w4 = sbuf([P, 2 * N], U8, "w4")
-        windows = [sbuf([P, T], F32, "window%d" % b) for b in range(3)]
+        windows = [sbuf([P, T], F32, "window%d" % b) for b in range(2)]
         gains = sbuf([P, J], F32, "gains")
         identity = sbuf([P, P], F32, "identity")
 
@@ -76,12 +76,9 @@ def tile_list_embg_mix_none_kernel(tc, dy, w8_words, w8_scales, w4_words, w4_sca
             nc.vector.tensor_tensor(windows[b][:].indirect(offsets[:, j0 // 16 : j1 // 16]), values, gains[:, j0:j1], MULT)
 
         make_identity(nc, identity[:])
-        for c0, c1 in ((0, 1023), (1023, T)):
+        for c0, c1 in ((0, 255), (255, 512), (512, T)):
             nc.vector.memset(windows[0][:, c0:c1].bitcast(I32), 0)
-        nc.gpsimd.memset(windows[1][:].bitcast(I32), 0)
-        for c0, c1 in ((0, 511), (511, 1024)):
-            nc.vector.memset(windows[2][:, c0:c1].bitcast(I32), 0)
-        nc.gpsimd.memset(windows[2][:, 1024:T].bitcast(I32), 0)
+        nc.vector.memset(windows[1][:].bitcast(I32), 0)
 
         load_dy(0, 0, CHUNK)
         load_scales(0, w8_scales)
@@ -136,6 +133,10 @@ def tile_list_embg_mix_none_kernel(tc, dy, w8_words, w8_scales, w4_words, w4_sca
             cols = slice(a * CHUNK, (a + 1) * CHUNK)
             interleave(nc.vector.tensor_copy, grouped0[:, a], a, 0, CHUNK)
             quantize(codes0[:, cols], scales0[:, cols], flat(grouped0[:, a : a + 1]))
+        window = sbuf([P, T], F32, "window2", "grouped0")
+        nc.vector.memset(window[:].bitcast(I32), 0)
+        windows.append(window)
+
         def f32_blocks(name, count, tag=None):
             return sbuf([P, count, P], F32, name, tag)
 

@@ -76,9 +76,11 @@ def tile_list_embg_mix_none_kernel(tc, dy, w8_words, w8_scales, w4_words, w4_sca
             nc.vector.tensor_tensor(windows[b][:].indirect(offsets[:, j0 // 16 : j1 // 16]), values, gains[:, j0:j1], MULT)
 
         make_identity(nc, identity[:])
-        for c0, c1 in ((0, 255), (255, 512), (512, T)):
+        for c0, c1 in ((0, 1023), (1023, T)):
             nc.vector.memset(windows[0][:, c0:c1].bitcast(I32), 0)
-        nc.vector.memset(windows[1][:].bitcast(I32), 0)
+        for c0, c1 in ((0, 159), (159, 320)):
+            nc.vector.memset(windows[1][:, c0:c1].bitcast(I32), 0)
+        nc.gpsimd.memset(windows[1][:, 320:T].bitcast(I32), 0)
 
         load_dy(0, 0, CHUNK)
         load_scales(0, w8_scales)
@@ -134,7 +136,9 @@ def tile_list_embg_mix_none_kernel(tc, dy, w8_words, w8_scales, w4_words, w4_sca
             interleave(nc.vector.tensor_copy, grouped0[:, a], a, 0, CHUNK)
             quantize(codes0[:, cols], scales0[:, cols], flat(grouped0[:, a : a + 1]))
         window = sbuf([P, T], F32, "window2", "grouped0")
-        nc.vector.memset(window[:].bitcast(I32), 0)
+        for c0, c1 in ((0, 511), (511, 1024)):
+            nc.vector.memset(window[:, c0:c1].bitcast(I32), 0)
+        nc.gpsimd.memset(window[:, 1024:T].bitcast(I32), 0)
         windows.append(window)
 
         def f32_blocks(name, count, tag=None):
@@ -170,8 +174,8 @@ def tile_list_embg_mix_none_kernel(tc, dy, w8_words, w8_scales, w4_words, w4_sca
         values01 = stage(back0, 1, 4, f32_blocks("values01", 3), 0)
 
         interleave(nc.vector.tensor_copy, grouped1[:, 0], 0, CHUNK, CHUNK)
-        quantize(codes1[:, 0:CHUNK], scales1[:, 0:CHUNK], flat(grouped1[:, 0:1]))
         interleave(nc.vector.tensor_copy, grouped1[:, 1], 1, CHUNK, CHUNK)
+        quantize(codes1[:, 0:CHUNK], scales1[:, 0:CHUNK], flat(grouped1[:, 0:1]))
         quantize(codes1[:, CHUNK:], scales1[:, CHUNK:], flat(grouped1[:, 1:2]))
         window = sbuf([P, T], F32, "window3", "grouped1")
         nc.gpsimd.memset(window[:].bitcast(I32), 0)
@@ -181,25 +185,25 @@ def tile_list_embg_mix_none_kernel(tc, dy, w8_words, w8_scales, w4_words, w4_sca
 
         rows1 = stage(multiply_chunk(1, codes1, scales1, (0, 1)), 0, 4, f32_blocks("rows1", 4), 0)
         back1 = turn_back("back1", rows1, 0, "back1")
-        grouped2 = round_on_scalar("grouped2", None, ((0, 2 * CHUNK), (1, 2 * CHUNK)), CHUNK)
+        grouped2 = round_on_scalar("grouped2", "rows0", ((0, 2 * CHUNK), (1, 2 * CHUNK)), CHUNK)
         values10 = stage(back1, 0, 2, f32_blocks("values10", 2, "raw1_256"), 0)
-        codes2, scales2 = new_codes("2", 2 * CHUNK, "values01")
+        codes2, scales2 = new_codes("2", 2 * CHUNK)
         quantize(codes2[:], scales2[:], flat(grouped2[:]))
         scatter_blocks(1, values10, 0)
 
-        grouped3 = round_on_scalar("grouped3", None, ((0, 3 * CHUNK), (1, 3 * CHUNK)), CHUNK)
-        low4 = round_on_scalar("low4", "grouped2", ((0, HALF),), PIECE)
+        grouped3 = round_on_scalar("grouped3", "codes1", ((0, 3 * CHUNK), (1, 3 * CHUNK)), CHUNK)
+        low4 = round_on_scalar("low4", "rows0", ((0, HALF),), PIECE)
         after4 = f32_blocks("after4", 6, "raw0_512")
         values12 = stage(back1, 2, 4, after4, 0)
         rows2 = stage(multiply_chunk(2, codes2, scales2, (0, 1)), 0, 4, after4, 2)
-        codes3, scales3 = new_codes("3", 2 * CHUNK, "raw1_256")
+        codes3, scales3 = new_codes("3", 2 * CHUNK)
         quantize(codes3[:], scales3[:], flat(grouped3[:]))
         low_codes, low_scales = new_codes("low", HALF)
         quantize(low_codes[:, 0:PIECE], low_scales[:, 0:PIECE], flat(low4[:]))
         scatter_blocks(1, values12, 2)
 
         back2 = turn_back("back2", rows2, 0, "back0")
-        low5 = round_on_scalar("low5", "grouped2", ((0, HALF + PIECE),), PIECE)
+        low5 = round_on_scalar("low5", "rows0", ((0, HALF + PIECE),), PIECE)
         values2 = f32_blocks("values2", 4)
         values20 = stage(back2, 0, 1, values2, 0)
         values21 = stage(back2, 1, 4, values2, 1)
@@ -208,11 +212,11 @@ def tile_list_embg_mix_none_kernel(tc, dy, w8_words, w8_scales, w4_words, w4_sca
 
         rows3 = stage(multiply_chunk(3, codes3, scales3, (0, 1)), 0, 4, f32_blocks("rows3", 4), 0)
         back3 = turn_back("back3", rows3, 0, "back1")
-        high = round_on_scalar("high", "raw1_256", ((1, HALF), (1, HALF + PIECE)), PIECE)
+        high = round_on_scalar("high", "codes3", ((1, HALF), (1, HALF + PIECE)), PIECE)
         values3 = f32_blocks("values3", 4, "raw1_768")
         values30 = stage(back3, 0, 1, values3, 0)
         values31 = stage(back3, 1, 4, values3, 1)
-        high_codes, high_scales = new_codes("high", HALF, "values2")
+        high_codes, high_scales = new_codes("high", HALF)
         quantize(high_codes[:], high_scales[:], flat(high[:]))
         scatter_blocks(3, values30 + values31, 0)
 

@@ -193,38 +193,39 @@ def tile_list_embg_mix_none_kernel(tc, dy, w8_words, w8_scales, w4_words, w4_sca
 
         grouped3 = round_on_scalar("grouped3", "codes1", ((0, 3 * CHUNK), (1, 3 * CHUNK)), CHUNK)
         low4 = round_on_scalar("low4", "rows0", ((0, HALF),), PIECE)
-        after4 = f32_blocks("after4", 6, "raw0_512")
-        values12 = stage(back1, 2, 4, after4, 0)
-        rows2 = stage(multiply_chunk(2, codes2, scales2, (0, 1)), 0, 4, after4, 2)
+        values12 = stage(back1, 2, 4, f32_blocks("values12", 2, "raw1_384"), 0)
+        rows2 = stage(multiply_chunk(2, codes2, scales2, (0, 1)), 0, 4, f32_blocks("rows2", 4, "raw0_512"), 0)
         codes3, scales3 = new_codes("3", 2 * CHUNK)
         quantize(codes3[:], scales3[:], flat(grouped3[:]))
-        low_codes, low_scales = new_codes("low", HALF)
-        quantize(low_codes[:, 0:PIECE], low_scales[:, 0:PIECE], flat(low4[:]))
         scatter_blocks(1, values12, 2)
 
         back2 = turn_back("back2", rows2, 0, "back0")
-        low5 = round_on_scalar("low5", "rows0", ((0, HALF + PIECE),), PIECE)
+        low5 = round_on_scalar("low5", "codes2", ((0, HALF + PIECE),), PIECE)
         values2 = f32_blocks("values2", 4)
         values20 = stage(back2, 0, 1, values2, 0)
         values21 = stage(back2, 1, 4, values2, 1)
-        quantize(low_codes[:, PIECE:], low_scales[:, PIECE:], flat(low5[:]))
         scatter_blocks(2, values20 + values21, 0)
 
         rows3 = stage(multiply_chunk(3, codes3, scales3, (0, 1)), 0, 4, f32_blocks("rows3", 4), 0)
         back3 = turn_back("back3", rows3, 0, "back1")
-        high = round_on_scalar("high", "codes3", ((1, HALF), (1, HALF + PIECE)), PIECE)
-        values3 = f32_blocks("values3", 4, "raw1_768")
-        values30 = stage(back3, 0, 1, values3, 0)
-        values31 = stage(back3, 1, 4, values3, 1)
+        high = sbuf([P, 2, PIECE, PACK], BF16, "high", "codes3")
+        interleave(nc.scalar.copy, high[:, 0], 1, HALF, PIECE)
+        values30 = stage(back3, 0, 1, f32_blocks("values30", 1), 0)
+        scatter_blocks(3, values30, 0)
+        interleave(nc.scalar.copy, high[:, 1], 1, HALF + PIECE, PIECE)
+        values31 = stage(back3, 1, 4, f32_blocks("values31", 3, "raw1_512"), 0)
+        low_codes, low_scales = new_codes("low", HALF, "raw1_768")
+        quantize(low_codes[:, 0:PIECE], low_scales[:, 0:PIECE], flat(low4[:]))
+        quantize(low_codes[:, PIECE:], low_scales[:, PIECE:], flat(low5[:]))
         high_codes, high_scales = new_codes("high", HALF)
         quantize(high_codes[:], high_scales[:], flat(high[:]))
-        scatter_blocks(3, values30 + values31, 0)
+        scatter_blocks(3, values31, 1)
 
         late_codes = [low_codes, high_codes]
         late_scales = [low_scales, high_scales]
         for b in range(BLOCKS):
             n0, n1 = b * P, (b + 1) * P
-            bank = psum.tile([P, HALF], F32, name="late%d" % b, tag="late%d" % b)
+            bank = psum.tile([P, HALF], F32, name="late%d" % b, tag="late")
             weights = [w8[:, n0:n1].bitcast(E4M3), w4[:, 2 * n0 : 2 * n1].bitcast(E2M1)]
             for a in range(2):
                 nc.tensor.matmul_mx(

@@ -78,9 +78,9 @@ def tile_list_embg_mix_none_kernel(tc, dy, w8_words, w8_scales, w4_words, w4_sca
         make_identity(nc, identity[:])
         for c0, c1 in ((0, 1023), (1023, T)):
             nc.vector.memset(windows[0][:, c0:c1].bitcast(I32), 0)
-        for c0, c1 in ((0, 159), (159, 320)):
+        for c0, c1 in ((0, 223), (223, 448)):
             nc.vector.memset(windows[1][:, c0:c1].bitcast(I32), 0)
-        nc.gpsimd.memset(windows[1][:, 320:T].bitcast(I32), 0)
+        nc.gpsimd.memset(windows[1][:, 448:T].bitcast(I32), 0)
 
         load_dy(0, 0, CHUNK)
         load_scales(0, w8_scales)
@@ -131,14 +131,14 @@ def tile_list_embg_mix_none_kernel(tc, dy, w8_words, w8_scales, w4_words, w4_sca
         grouped1 = sbuf([P, 2, CHUNK, PACK], BF16, "grouped1")
         codes0, scales0 = new_codes("0", 2 * CHUNK)
         codes1, scales1 = new_codes("1", 2 * CHUNK)
-        for a in range(2):
+        for a, engine_copy in enumerate((nc.scalar.copy, nc.vector.tensor_copy)):
             cols = slice(a * CHUNK, (a + 1) * CHUNK)
-            interleave(nc.vector.tensor_copy, grouped0[:, a], a, 0, CHUNK)
+            interleave(engine_copy, grouped0[:, a], a, 0, CHUNK)
             quantize(codes0[:, cols], scales0[:, cols], flat(grouped0[:, a : a + 1]))
         window = sbuf([P, T], F32, "window2", "grouped0")
-        for c0, c1 in ((0, 511), (511, 1024)):
+        for c0, c1 in ((0, 575), (575, 1152)):
             nc.vector.memset(window[:, c0:c1].bitcast(I32), 0)
-        nc.gpsimd.memset(window[:, 1024:T].bitcast(I32), 0)
+        nc.gpsimd.memset(window[:, 1152:T].bitcast(I32), 0)
         windows.append(window)
 
         def f32_blocks(name, count, tag=None):
@@ -183,7 +183,7 @@ def tile_list_embg_mix_none_kernel(tc, dy, w8_words, w8_scales, w4_words, w4_sca
         scatter_blocks(0, values00, 0)
         scatter_blocks(0, values01, 1)
 
-        rows1 = stage(multiply_chunk(1, codes1, scales1, (0, 1)), 0, 4, f32_blocks("rows1", 4), 0)
+        rows1 = stage(multiply_chunk(1, codes1, scales1, (0, 1)), 0, 4, f32_blocks("rows1", 4, "raw0_256"), 0)
         back1 = turn_back("back1", rows1, 0, "back1")
         grouped2 = round_on_scalar("grouped2", "rows0", ((0, 2 * CHUNK), (1, 2 * CHUNK)), CHUNK)
         values10 = stage(back1, 0, 2, f32_blocks("values10", 2, "raw1_256"), 0)

@@ -105,11 +105,11 @@ def tile_list_embg_mix_none_kernel(tc, dy, w8_words, w8_scales, w4_words, w4_sca
         def flat(grouped):
             return grouped.rearrange("p a j t -> p (a j t)")
 
-        def multiply_chunk(c, codes, scales, order):
-            bank = psum.tile([P, N], F32, name="tokens%d" % c, tag="tokens")
+        def multiply_chunk(c, codes, scales, tag):
+            bank = psum.tile([P, N], F32, name="tokens%d" % c, tag=tag)
             moving = [w8[:].bitcast(E4M3), w4[:].bitcast(E2M1)]
             for a in range(2):
-                cols = slice(order[a] * CHUNK, (order[a] + 1) * CHUNK)
+                cols = slice(a * CHUNK, (a + 1) * CHUNK)
                 nc.tensor.matmul_mx(
                     out=bank[:],
                     lhsT=codes[:, cols].bitcast(E5M2),
@@ -164,7 +164,7 @@ def tile_list_embg_mix_none_kernel(tc, dy, w8_words, w8_scales, w4_words, w4_sca
                 interleave(nc.scalar.copy, tile[:, i], a, j0, width)
             return tile
 
-        bank = multiply_chunk(0, codes0, scales0, (0, 1))
+        bank = multiply_chunk(0, codes0, scales0, "tokens")
         rows0 = f32_blocks("rows0", 4)
         lead = stage(bank, 0, 1, rows0, 0)
         others = stage(bank, 1, 4, rows0, 1)
@@ -183,42 +183,62 @@ def tile_list_embg_mix_none_kernel(tc, dy, w8_words, w8_scales, w4_words, w4_sca
         scatter_blocks(0, values00, 0)
         scatter_blocks(0, values01, 1)
 
-        rows1 = stage(multiply_chunk(1, codes1, scales1, (0, 1)), 0, 4, f32_blocks("rows1", 4, "raw0_256"), 0)
-        back1 = turn_back("back1", rows1, 0, "back1")
-        grouped2 = round_on_scalar("grouped2", "rows0", ((0, 2 * CHUNK), (1, 2 * CHUNK)), CHUNK)
-        values10 = stage(back1, 0, 2, f32_blocks("values10", 2, "raw1_256"), 0)
+        grouped2 = sbuf([P, 2, CHUNK, PACK], BF16, "grouped2", "rows0")
+        interleave(nc.scalar.copy, grouped2[:, 0], 0, 2 * CHUNK, CHUNK)
+        rows1 = stage(multiply_chunk(1, codes1, scales1, "tokens"), 0, 4, f32_blocks("rows1", 4, "raw0_256"), 0)
+        front1 = turn_back("front1", rows1[0:2], 0, "first")
+        back1 = turn_back("back1", rows1[2:4], 2, "back1")
+        interleave(nc.scalar.copy, grouped2[:, 1], 1, 2 * CHUNK, CHUNK)
+        grouped3 = sbuf([P, 2, CHUNK, PACK], BF16, "grouped3", "codes1")
+        interleave(nc.scalar.copy, grouped3[:, 0], 0, 3 * CHUNK, CHUNK)
+        values10 = stage(front1, 0, 2, f32_blocks("values10", 2, "raw1_256"), 0)
         codes2, scales2 = new_codes("2", 2 * CHUNK)
         quantize(codes2[:], scales2[:], flat(grouped2[:]))
         scatter_blocks(1, values10, 0)
-
-        grouped3 = round_on_scalar("grouped3", "codes1", ((0, 3 * CHUNK), (1, 3 * CHUNK)), CHUNK)
-        low4 = round_on_scalar("low4", "rows0", ((0, HALF),), PIECE)
+        interleave(nc.scalar.copy, grouped3[:, 1], 1, 3 * CHUNK, CHUNK)
         values12 = stage(back1, 2, 4, f32_blocks("values12", 2, "raw1_384"), 0)
-        rows2 = stage(multiply_chunk(2, codes2, scales2, (0, 1)), 0, 4, f32_blocks("rows2", 4, "raw0_512"), 0)
         codes3, scales3 = new_codes("3", 2 * CHUNK)
         quantize(codes3[:], scales3[:], flat(grouped3[:]))
         scatter_blocks(1, values12, 2)
 
-        back2 = turn_back("back2", rows2, 0, "back0")
-        low5 = round_on_scalar("low5", "codes2", ((0, HALF + PIECE),), PIECE)
-        values2 = f32_blocks("values2", 4)
-        values20 = stage(back2, 0, 1, values2, 0)
-        values21 = stage(back2, 1, 4, values2, 1)
+        late = sbuf([P, 2 * HALF * PACK], BF16, "late", "rows0")
+
+        def round_late(a, j0, width):
+            c0 = (a * HALF + j0) * PACK
+            piece = late[:, c0 : c0 + width * PACK].rearrange("p (j t) -> p j t", t=PACK)
+            interleave(nc.scalar.copy, piece, a, HALF + j0, width)
+
+        def across(a, j0):
+            c0 = (a * HALF + j0) * PACK
+            return late[:, c0 - P : c0 + P].bitcast(F32).rearrange("p (b c) -> p b c", c=P)
+
+        round_late(0, 0, CHUNK)
+        bank = multiply_chunk(2, codes2, scales2, "first")
+        lead = stage(bank, 0, 1, across(1, 0), 0)
+        others = stage(bank, 1, 4, late[:, PIECE * PACK : PIECE * PACK + 6 * P].bitcast(F32).rearrange("p (b c) -> p b c", c=P), 0)
+        front2 = turn_back("front2", lead, 0, "tokens")
+        back2 = turn_back("back2", others, 1, "back0")
+        round_late(0, CHUNK, CHUNK)
+        values20 = stage(front2, 0, 1, f32_blocks("values20", 1), 0)
+        values21 = stage(back2, 1, 4, f32_blocks("values21", 3), 0)
         scatter_blocks(2, values20 + values21, 0)
 
-        rows3 = stage(multiply_chunk(3, codes3, scales3, (0, 1)), 0, 4, f32_blocks("rows3", 4), 0)
-        back3 = turn_back("back3", rows3, 0, "back1")
-        high = sbuf([P, 2, PIECE, PACK], BF16, "high", "codes3")
-        interleave(nc.scalar.copy, high[:, 0], 1, HALF, PIECE)
-        values30 = stage(back3, 0, 1, f32_blocks("values30", 1), 0)
+        round_late(0, PIECE, PIECE)
+        bank = multiply_chunk(3, codes3, scales3, "tokens")
+        lead = stage(bank, 0, 1, across(1, PIECE), 0)
+        others = stage(bank, 1, 4, f32_blocks("others3", 3), 0)
+        front3 = turn_back("front3", lead, 0, "first")
+        back3 = turn_back("back3", others, 1, "back1")
+        round_late(1, 0, CHUNK)
+        values30 = stage(front3, 0, 1, f32_blocks("values30", 1), 0)
         scatter_blocks(3, values30, 0)
-        interleave(nc.scalar.copy, high[:, 1], 1, HALF + PIECE, PIECE)
+        round_late(1, CHUNK, CHUNK)
+        round_late(1, PIECE, PIECE)
         values31 = stage(back3, 1, 4, f32_blocks("values31", 3, "raw1_512"), 0)
-        low_codes, low_scales = new_codes("low", HALF, "raw1_768")
-        quantize(low_codes[:, 0:PIECE], low_scales[:, 0:PIECE], flat(low4[:]))
-        quantize(low_codes[:, PIECE:], low_scales[:, PIECE:], flat(low5[:]))
+        low_codes, low_scales = new_codes("low", HALF)
+        quantize(low_codes[:], low_scales[:], late[:, 0 : HALF * PACK])
         high_codes, high_scales = new_codes("high", HALF)
-        quantize(high_codes[:], high_scales[:], flat(high[:]))
+        quantize(high_codes[:], high_scales[:], late[:, HALF * PACK :])
         scatter_blocks(3, values31, 1)
 
         late_codes = [low_codes, high_codes]

@@ -20,10 +20,14 @@ MULT = mybir.AluOpType.mult
 P = 128
 PACK = 4
 K_PASS = P * PACK
-HALF = 512
-BLOCKS = N // P
+GROUPS = N // P
+LIST_ROWS = 16
 CHUNK = 128
+HALF = 512
 PIECE = 256
+LOW, HIGH = 0, 1
+VECTOR_ZEROES_1 = 448
+VECTOR_ZEROES_2 = 1152
 
 
 def tile_list_embg_mix_none_kernel(tc, dy, w8_words, w8_scales, w4_words, w4_scales, wgo, offs, out):
@@ -32,21 +36,23 @@ def tile_list_embg_mix_none_kernel(tc, dy, w8_words, w8_scales, w4_words, w4_sca
         keep = ctx.enter_context(tc.tile_pool(name="keep", bufs=1))
         psum = ctx.enter_context(tc.psum_pool(name="psum", bufs=1))
 
-        def sbuf(shape, dtype, name, tag=None):
-            return keep.tile(shape, dtype, name=name, tag=tag or name, align_bytes=64)
+        def sbuf(shape, dtype, name, on=None):
+            return keep.tile(shape, dtype, name=name, tag=on or name, align_bytes=64)
 
-        offsets = keep.tile([P, J // 16], U16, name="offsets")
+        offsets = keep.tile([P, J // LIST_ROWS], U16, name="offsets")
         w_scales = sbuf([P, 2 * N], U8, "w_scales")
         w8 = sbuf([P, N], U32, "w8")
         w4 = sbuf([P, 2 * N], U8, "w4")
         windows = [sbuf([P, T], F32, "window%d" % b) for b in range(2)]
         gains = sbuf([P, J], F32, "gains")
         identity = sbuf([P, P], F32, "identity")
-
         raw = {}
 
+        def raw_name(a, j0):
+            return "raw%d_%d" % (a, j0)
+
         def load_dy(a, j0, j1):
-            tile = sbuf([P, PACK, j1 - j0], F32, "raw%d_%d" % (a, j0))
+            tile = sbuf([P, PACK, j1 - j0], F32, raw_name(a, j0))
             rows = dy[a * K_PASS : (a + 1) * K_PASS, j0:j1]
             nc.sync.dma_start(out=tile[:], in_=rows.rearrange("(p t) j -> p t j", t=PACK))
             for j in range(j0, j1, CHUNK):
@@ -62,202 +68,202 @@ def tile_list_embg_mix_none_kernel(tc, dy, w8_words, w8_scales, w4_words, w4_sca
         def load_gains(j0, j1):
             nc.sync.dma_start(out=gains[:, j0:j1], in_=wgo[:, j0:j1])
 
-        def interleave(engine_copy, grouped, a, j0, width):
+        def zero_on_vector(window, width):
+            cut = width // 2 - 1
+            for c0, c1 in ((0, cut), (cut, width)):
+                nc.vector.memset(window[:, c0:c1].bitcast(I32), 0)
+
+        def zero_on_both(window, vector_share):
+            zero_on_vector(window, vector_share)
+            nc.gpsimd.memset(window[:, vector_share:T].bitcast(I32), 0)
+
+        def interleave(engine_copy, rounded, a, j0, width):
             tile, c0 = raw[a, j0]
             engine_copy(
-                out=grouped.rearrange("p (c i) t -> p c t i", i=4),
+                out=rounded.rearrange("p (c i) t -> p c t i", i=4),
                 in_=tile[:, :, c0 : c0 + width].rearrange("p t (c i) -> p c t i", i=4),
             )
 
-        def quantize(codes, scales, grouped):
-            nc.vector.quantize_mx(out=codes.bitcast(E5M2), scales=scales, in_=grouped)
+        def new_rounded(name, on=None):
+            return sbuf([P, 2, CHUNK, PACK], BF16, name, on)
 
-        def scatter(b, values, j0, j1):
-            nc.vector.tensor_tensor(windows[b][:].indirect(offsets[:, j0 // 16 : j1 // 16]), values, gains[:, j0:j1], MULT)
+        def flat(rounded):
+            return rounded.rearrange("p a j t -> p (a j t)")
 
-        make_identity(nc, identity[:])
-        for c0, c1 in ((0, 1023), (1023, T)):
-            nc.vector.memset(windows[0][:, c0:c1].bitcast(I32), 0)
-        for c0, c1 in ((0, 223), (223, 448)):
-            nc.vector.memset(windows[1][:, c0:c1].bitcast(I32), 0)
-        nc.gpsimd.memset(windows[1][:, 448:T].bitcast(I32), 0)
+        def new_codes(name, width):
+            return sbuf([P, width], U32, "codes" + name), sbuf([P, width], U8, "scales" + name)
 
-        load_dy(0, 0, CHUNK)
-        load_scales(0, w8_scales)
-        load_dy(1, 0, CHUNK)
-        nc.sync.dma_start(out=w8[:].bitcast(I32), in_=w8_words[0].rearrange("p n t -> p (n t)").bitcast(I32))
-        nc.sync.dma_start(out=w4[:].bitcast(I32), in_=w4_words[0].bitcast(I32))
-        load_scales(1, w4_scales)
-        load_dy(0, CHUNK, 2 * CHUNK)
-        load_dy(1, CHUNK, 2 * CHUNK)
-        nc.sync.dma_start(offsets[:], offs)
-        load_gains(0, 2 * CHUNK)
-        for c in (2, 3):
-            load_dy(0, c * CHUNK, (c + 1) * CHUNK)
-            load_dy(1, c * CHUNK, (c + 1) * CHUNK)
-        load_dy(0, HALF, HALF + PIECE)
-        load_gains(2 * CHUNK, HALF)
-        load_dy(0, HALF + PIECE, J)
-        load_dy(1, HALF, HALF + PIECE)
-        load_dy(1, HALF + PIECE, J)
-        load_gains(HALF, J)
+        def quantize(codes, scales, rounded):
+            nc.vector.quantize_mx(out=codes.bitcast(E5M2), scales=scales, in_=rounded)
 
-        def flat(grouped):
-            return grouped.rearrange("p a j t -> p (a j t)")
-
-        def multiply_chunk(c, codes, scales, tag):
-            bank = psum.tile([P, N], F32, name="tokens%d" % c, tag=tag)
-            moving = [w8[:].bitcast(E4M3), w4[:].bitcast(E2M1)]
-            for a in range(2):
+        def multiply_chunk(c, codes, scales, bank_tag):
+            bank = psum.tile([P, N], F32, name="product%d" % c, tag=bank_tag)
+            weights = [w8[:].bitcast(E4M3), w4[:].bitcast(E2M1)]
+            for a in (LOW, HIGH):
                 cols = slice(a * CHUNK, (a + 1) * CHUNK)
                 nc.tensor.matmul_mx(
                     out=bank[:],
                     lhsT=codes[:, cols].bitcast(E5M2),
                     lhsT_scale=scales[:, cols],
-                    rhs=moving[a],
+                    rhs=weights[a],
                     rhs_scale=w_scales[:, a * N : (a + 1) * N],
-                    start=a == 0,
-                    stop=a == 1,
+                    start=a == LOW,
+                    stop=a == HIGH,
                 )
             return bank
 
-        def by_block(bank, b0, b1):
-            return bank[:, b0 * P : b1 * P].rearrange("p (b c) -> p b c", c=P)
+        def new_squares(name, count, on=None):
+            return sbuf([P, count, P], F32, name, on)
 
-        def new_codes(name, width, tag=None):
-            return sbuf([P, width], U32, "codes" + name, tag), sbuf([P, width], U8, "scales" + name)
+        def copy_out(bank, b0, b1, squares):
+            nc.scalar.copy(out=squares, in_=bank[:, b0 * P : b1 * P].rearrange("p (b c) -> p b c", c=P))
+            return [squares[:, i, :] for i in range(b1 - b0)]
 
-        grouped0 = sbuf([P, 2, CHUNK, PACK], BF16, "grouped0")
-        grouped1 = sbuf([P, 2, CHUNK, PACK], BF16, "grouped1")
+        def turn(name, by_token, b0, bank_tag):
+            bank = psum.tile([P, N], F32, name=name, tag=bank_tag)
+            for i, square in enumerate(by_token):
+                nc.tensor.transpose(bank[:, (b0 + i) * P : (b0 + i + 1) * P], square, identity[:])
+            return bank
+
+        def scatter(b, values, j0, j1):
+            places = windows[b][:].indirect(offsets[:, j0 // LIST_ROWS : j1 // LIST_ROWS])
+            nc.vector.tensor_tensor(places, values, gains[:, j0:j1], MULT)
+
+        def scatter_chunk(c, values, b0):
+            for i, square in enumerate(values):
+                scatter(b0 + i, square, c * CHUNK, (c + 1) * CHUNK)
+
+        make_identity(nc, identity[:])
+        zero_on_vector(windows[0], T)
+        zero_on_both(windows[1], VECTOR_ZEROES_1)
+
+        load_dy(LOW, 0, CHUNK)
+        load_scales(LOW, w8_scales)
+        load_dy(HIGH, 0, CHUNK)
+        nc.sync.dma_start(out=w8[:].bitcast(I32), in_=w8_words[0].rearrange("p n t -> p (n t)").bitcast(I32))
+        nc.sync.dma_start(out=w4[:].bitcast(I32), in_=w4_words[0].bitcast(I32))
+        load_scales(HIGH, w4_scales)
+        load_dy(LOW, CHUNK, 2 * CHUNK)
+        load_dy(HIGH, CHUNK, 2 * CHUNK)
+        nc.sync.dma_start(offsets[:], offs)
+        load_gains(0, 2 * CHUNK)
+        for c in (2, 3):
+            load_dy(LOW, c * CHUNK, (c + 1) * CHUNK)
+            load_dy(HIGH, c * CHUNK, (c + 1) * CHUNK)
+        load_dy(LOW, HALF, HALF + PIECE)
+        load_gains(2 * CHUNK, HALF)
+        load_dy(LOW, HALF + PIECE, J)
+        load_dy(HIGH, HALF, HALF + PIECE)
+        load_dy(HIGH, HALF + PIECE, J)
+        load_gains(HALF, J)
+
+        rounded0 = new_rounded("rounded0")
+        rounded1 = new_rounded("rounded1")
         codes0, scales0 = new_codes("0", 2 * CHUNK)
         codes1, scales1 = new_codes("1", 2 * CHUNK)
-        for a, engine_copy in enumerate((nc.scalar.copy, nc.vector.tensor_copy)):
+        for a, engine_copy in ((LOW, nc.scalar.copy), (HIGH, nc.vector.tensor_copy)):
             cols = slice(a * CHUNK, (a + 1) * CHUNK)
-            interleave(engine_copy, grouped0[:, a], a, 0, CHUNK)
-            quantize(codes0[:, cols], scales0[:, cols], flat(grouped0[:, a : a + 1]))
-        window = sbuf([P, T], F32, "window2", "grouped0")
-        for c0, c1 in ((0, 575), (575, 1152)):
-            nc.vector.memset(window[:, c0:c1].bitcast(I32), 0)
-        nc.gpsimd.memset(window[:, 1152:T].bitcast(I32), 0)
-        windows.append(window)
+            interleave(engine_copy, rounded0[:, a], a, 0, CHUNK)
+            quantize(codes0[:, cols], scales0[:, cols], flat(rounded0[:, a : a + 1]))
+        windows.append(sbuf([P, T], F32, "window2", "rounded0"))
+        zero_on_both(windows[2], VECTOR_ZEROES_2)
+        product = multiply_chunk(0, codes0, scales0, "bank_a")
+        by_token0 = new_squares("by_token0", GROUPS)
+        lead = copy_out(product, 0, 1, by_token0[:, 0:1, :])
+        others = copy_out(product, 1, GROUPS, by_token0[:, 1:GROUPS, :])
+        turned_lead = turn("lead0", lead, 0, "bank_b")
+        turned_others = turn("others0", others, 1, "bank_c")
+        values_lead = copy_out(turned_lead, 0, 1, new_squares("values00", 1)[:])
+        values_others = copy_out(turned_others, 1, GROUPS, new_squares("values01", GROUPS - 1)[:])
 
-        def f32_blocks(name, count, tag=None):
-            return sbuf([P, count, P], F32, name, tag)
+        for a in (LOW, HIGH):
+            interleave(nc.vector.tensor_copy, rounded1[:, a], a, CHUNK, CHUNK)
+        for a in (LOW, HIGH):
+            cols = slice(a * CHUNK, (a + 1) * CHUNK)
+            quantize(codes1[:, cols], scales1[:, cols], flat(rounded1[:, a : a + 1]))
+        windows.append(sbuf([P, T], F32, "window3", "rounded1"))
+        nc.gpsimd.memset(windows[3][:].bitcast(I32), 0)
+        scatter_chunk(0, values_lead, 0)
+        scatter_chunk(0, values_others, 1)
 
-        def stage(bank, b0, b1, tile, slot):
-            nc.scalar.copy(out=tile[:, slot : slot + b1 - b0, :], in_=by_block(bank, b0, b1))
-            return [tile[:, slot + i, :] for i in range(b1 - b0)]
-
-        def turn_back(name, rows, b0, tag):
-            back = psum.tile([P, N], F32, name=name, tag=tag)
-            for i, block in enumerate(rows):
-                nc.tensor.transpose(back[:, (b0 + i) * P : (b0 + i + 1) * P], block, identity[:])
-            return back
-
-        def scatter_blocks(c, values, b0):
-            for i, block in enumerate(values):
-                scatter(b0 + i, block, c * CHUNK, (c + 1) * CHUNK)
-
-        def round_on_scalar(name, tag, pieces, width):
-            tile = sbuf([P, len(pieces), width, PACK], BF16, name, tag)
-            for i, (a, j0) in enumerate(pieces):
-                interleave(nc.scalar.copy, tile[:, i], a, j0, width)
-            return tile
-
-        bank = multiply_chunk(0, codes0, scales0, "tokens")
-        rows0 = f32_blocks("rows0", 4)
-        lead = stage(bank, 0, 1, rows0, 0)
-        others = stage(bank, 1, 4, rows0, 1)
-        first = turn_back("first0", lead, 0, "first")
-        back0 = turn_back("back0", others, 1, "back0")
-        values00 = stage(first, 0, 1, f32_blocks("values00", 1), 0)
-        values01 = stage(back0, 1, 4, f32_blocks("values01", 3), 0)
-
-        interleave(nc.vector.tensor_copy, grouped1[:, 0], 0, CHUNK, CHUNK)
-        interleave(nc.vector.tensor_copy, grouped1[:, 1], 1, CHUNK, CHUNK)
-        quantize(codes1[:, 0:CHUNK], scales1[:, 0:CHUNK], flat(grouped1[:, 0:1]))
-        quantize(codes1[:, CHUNK:], scales1[:, CHUNK:], flat(grouped1[:, 1:2]))
-        window = sbuf([P, T], F32, "window3", "grouped1")
-        nc.gpsimd.memset(window[:].bitcast(I32), 0)
-        windows.append(window)
-        scatter_blocks(0, values00, 0)
-        scatter_blocks(0, values01, 1)
-
-        grouped2 = sbuf([P, 2, CHUNK, PACK], BF16, "grouped2", "rows0")
-        interleave(nc.scalar.copy, grouped2[:, 0], 0, 2 * CHUNK, CHUNK)
-        rows1 = stage(multiply_chunk(1, codes1, scales1, "tokens"), 0, 4, f32_blocks("rows1", 4, "raw0_256"), 0)
-        front1 = turn_back("front1", rows1[0:2], 0, "first")
-        back1 = turn_back("back1", rows1[2:4], 2, "back1")
-        interleave(nc.scalar.copy, grouped2[:, 1], 1, 2 * CHUNK, CHUNK)
-        grouped3 = sbuf([P, 2, CHUNK, PACK], BF16, "grouped3", "codes1")
-        interleave(nc.scalar.copy, grouped3[:, 0], 0, 3 * CHUNK, CHUNK)
-        values10 = stage(front1, 0, 2, f32_blocks("values10", 2, "raw1_256"), 0)
+        rounded2 = new_rounded("rounded2", "by_token0")
+        interleave(nc.scalar.copy, rounded2[:, LOW], LOW, 2 * CHUNK, CHUNK)
+        product = multiply_chunk(1, codes1, scales1, "bank_a")
+        by_token1 = copy_out(product, 0, GROUPS, new_squares("by_token1", GROUPS, raw_name(LOW, 2 * CHUNK))[:])
+        turned_front = turn("front1", by_token1[0:2], 0, "bank_b")
+        turned_back = turn("back1", by_token1[2:GROUPS], 2, "bank_d")
+        interleave(nc.scalar.copy, rounded2[:, HIGH], HIGH, 2 * CHUNK, CHUNK)
+        rounded3 = new_rounded("rounded3", "codes1")
+        interleave(nc.scalar.copy, rounded3[:, LOW], LOW, 3 * CHUNK, CHUNK)
+        values_front = copy_out(turned_front, 0, 2, new_squares("values10", 2, raw_name(HIGH, 2 * CHUNK))[:])
         codes2, scales2 = new_codes("2", 2 * CHUNK)
-        quantize(codes2[:], scales2[:], flat(grouped2[:]))
-        scatter_blocks(1, values10, 0)
-        interleave(nc.scalar.copy, grouped3[:, 1], 1, 3 * CHUNK, CHUNK)
-        values12 = stage(back1, 2, 4, f32_blocks("values12", 2, "raw1_384"), 0)
+        quantize(codes2[:], scales2[:], flat(rounded2[:]))
+        scatter_chunk(1, values_front, 0)
+        interleave(nc.scalar.copy, rounded3[:, HIGH], HIGH, 3 * CHUNK, CHUNK)
+        values_back = copy_out(turned_back, 2, GROUPS, new_squares("values12", 2, raw_name(HIGH, 3 * CHUNK))[:])
         codes3, scales3 = new_codes("3", 2 * CHUNK)
-        quantize(codes3[:], scales3[:], flat(grouped3[:]))
-        scatter_blocks(1, values12, 2)
+        quantize(codes3[:], scales3[:], flat(rounded3[:]))
+        scatter_chunk(1, values_back, 2)
 
-        late = sbuf([P, 2 * HALF * PACK], BF16, "late", "rows0")
+        late = sbuf([P, 2 * HALF * PACK], BF16, "late", "by_token0")
+
+        def late_column(a, j):
+            return (a * HALF + j) * PACK
 
         def round_late(a, j0, width):
-            c0 = (a * HALF + j0) * PACK
-            piece = late[:, c0 : c0 + width * PACK].rearrange("p (j t) -> p j t", t=PACK)
-            interleave(nc.scalar.copy, piece, a, HALF + j0, width)
+            piece = late[:, late_column(a, j0) : late_column(a, j0 + width)]
+            interleave(nc.scalar.copy, piece.rearrange("p (j t) -> p j t", t=PACK), a, HALF + j0, width)
 
-        def across(a, j0):
-            c0 = (a * HALF + j0) * PACK
-            return late[:, c0 - P : c0 + P].bitcast(F32).rearrange("p (b c) -> p b c", c=P)
+        def squares_on_late(c0, count):
+            return late[:, c0 : c0 + 2 * P * count].bitcast(F32).rearrange("p (b c) -> p b c", c=P)
 
-        round_late(0, 0, CHUNK)
-        bank = multiply_chunk(2, codes2, scales2, "first")
-        lead = stage(bank, 0, 1, across(1, 0), 0)
-        others = stage(bank, 1, 4, late[:, PIECE * PACK : PIECE * PACK + 6 * P].bitcast(F32).rearrange("p (b c) -> p b c", c=P), 0)
-        front2 = turn_back("front2", lead, 0, "tokens")
-        back2 = turn_back("back2", others, 1, "back0")
-        round_late(0, CHUNK, CHUNK)
-        values20 = stage(front2, 0, 1, f32_blocks("values20", 1), 0)
-        values21 = stage(back2, 1, 4, f32_blocks("values21", 3), 0)
-        scatter_blocks(2, values20 + values21, 0)
+        round_late(LOW, 0, CHUNK)
+        product = multiply_chunk(2, codes2, scales2, "bank_b")
+        lead = copy_out(product, 0, 1, squares_on_late(late_column(HIGH, 0) - P, 1))
+        others = copy_out(product, 1, GROUPS, squares_on_late(late_column(LOW, PIECE), GROUPS - 1))
+        turned_lead = turn("lead2", lead, 0, "bank_a")
+        turned_others = turn("others2", others, 1, "bank_c")
+        round_late(LOW, CHUNK, CHUNK)
+        values_lead = copy_out(turned_lead, 0, 1, new_squares("values20", 1)[:])
+        values_others = copy_out(turned_others, 1, GROUPS, new_squares("values21", GROUPS - 1)[:])
+        scatter_chunk(2, values_lead + values_others, 0)
 
-        round_late(0, PIECE, PIECE)
-        bank = multiply_chunk(3, codes3, scales3, "tokens")
-        lead = stage(bank, 0, 1, across(1, PIECE), 0)
-        others = stage(bank, 1, 4, f32_blocks("others3", 3), 0)
-        front3 = turn_back("front3", lead, 0, "first")
-        back3 = turn_back("back3", others, 1, "back1")
-        round_late(1, 0, CHUNK)
-        values30 = stage(front3, 0, 1, f32_blocks("values30", 1), 0)
-        scatter_blocks(3, values30, 0)
-        round_late(1, CHUNK, CHUNK)
-        round_late(1, PIECE, PIECE)
-        values31 = stage(back3, 1, 4, f32_blocks("values31", 3, "raw1_512"), 0)
-        low_codes, low_scales = new_codes("low", HALF)
-        quantize(low_codes[:], low_scales[:], late[:, 0 : HALF * PACK])
-        high_codes, high_scales = new_codes("high", HALF)
-        quantize(high_codes[:], high_scales[:], late[:, HALF * PACK :])
-        scatter_blocks(3, values31, 1)
+        round_late(LOW, PIECE, PIECE)
+        product = multiply_chunk(3, codes3, scales3, "bank_a")
+        lead = copy_out(product, 0, 1, squares_on_late(late_column(HIGH, PIECE) - P, 1))
+        others = copy_out(product, 1, GROUPS, new_squares("by_token3", GROUPS - 1)[:])
+        turned_lead = turn("lead3", lead, 0, "bank_b")
+        turned_others = turn("others3", others, 1, "bank_d")
+        round_late(HIGH, 0, CHUNK)
+        values_lead = copy_out(turned_lead, 0, 1, new_squares("values30", 1)[:])
+        scatter_chunk(3, values_lead, 0)
+        round_late(HIGH, CHUNK, CHUNK)
+        round_late(HIGH, PIECE, PIECE)
+        values_others = copy_out(turned_others, 1, GROUPS, new_squares("values31", GROUPS - 1, raw_name(HIGH, HALF))[:])
+        late_codes = []
+        for a, name in ((LOW, "low"), (HIGH, "high")):
+            codes, scales = new_codes(name, HALF)
+            quantize(codes[:], scales[:], late[:, late_column(a, 0) : late_column(a, HALF)])
+            late_codes.append((codes, scales))
+        scatter_chunk(3, values_others, 1)
 
-        late_codes = [low_codes, high_codes]
-        late_scales = [low_scales, high_scales]
-        for b in range(BLOCKS):
+        for b in range(GROUPS):
             n0, n1 = b * P, (b + 1) * P
-            bank = psum.tile([P, HALF], F32, name="late%d" % b, tag="late")
+            product = psum.tile([P, HALF], F32, name="late_product%d" % b, tag="bank_late")
             weights = [w8[:, n0:n1].bitcast(E4M3), w4[:, 2 * n0 : 2 * n1].bitcast(E2M1)]
-            for a in range(2):
+            for a in (LOW, HIGH):
+                codes, scales = late_codes[a]
                 nc.tensor.matmul_mx(
-                    out=bank[:],
+                    out=product[:],
                     lhsT=weights[a],
                     lhsT_scale=w_scales[:, a * N + n0 : a * N + n1],
-                    rhs=late_codes[a][:].bitcast(E5M2),
-                    rhs_scale=late_scales[a][:],
-                    start=a == 0,
-                    stop=a == 1,
+                    rhs=codes[:].bitcast(E5M2),
+                    rhs_scale=scales[:],
+                    start=a == LOW,
+                    stop=a == HIGH,
                 )
-            staged = sbuf([P, HALF], F32, "late_staged%d" % b)
-            nc.scalar.copy(out=staged[:], in_=bank[:])
-            scatter(b, staged[:], HALF, J)
-            nc.sync.dma_start(out=out[n0:n1, :], in_=windows[b][:])
+            values = sbuf([P, HALF], F32, "late_values%d" % b)
+            nc.scalar.copy(out=values[:], in_=product[:])
+            scatter(b, values[:], HALF, J)
+            for c0, c1 in ((0, T // 2), (T // 2, T)) if b == GROUPS - 1 else ((0, T),):
+                nc.sync.dma_start(out=out[n0:n1, c0:c1], in_=windows[b][:, c0:c1])

@@ -1,7 +1,6 @@
 from contextlib import ExitStack
 
 import concourse.mybir as mybir
-from concourse.masks import make_identity
 
 K, N, T, J = 1024, 512, 2048, 1024
 FLOPS = 2 * K * N * J
@@ -22,12 +21,7 @@ PACK = 4
 K_PASS = P * PACK
 GROUPS = N // P
 LIST_ROWS = 16
-CHUNK = 128
-HALF = 512
-PIECE = 256
 LOW, HIGH = 0, 1
-VECTOR_ZEROES_1 = 448
-VECTOR_ZEROES_2 = 1152
 
 
 def tile_list_embg_mix_none_kernel(tc, dy, w8_words, w8_scales, w4_words, w4_scales, wgo, offs, out):
@@ -43,9 +37,8 @@ def tile_list_embg_mix_none_kernel(tc, dy, w8_words, w8_scales, w4_words, w4_sca
         w_scales = sbuf([P, 2 * N], U8, "w_scales")
         w8 = sbuf([P, N], U32, "w8")
         w4 = sbuf([P, 2 * N], U8, "w4")
-        windows = [sbuf([P, T], F32, "window%d" % b) for b in range(2)]
         gains = sbuf([P, J], F32, "gains")
-        identity = sbuf([P, P], F32, "identity")
+        windows = {}
         raw = {}
 
         def raw_name(a, j0):
@@ -55,7 +48,7 @@ def tile_list_embg_mix_none_kernel(tc, dy, w8_words, w8_scales, w4_words, w4_sca
             tile = sbuf([P, PACK, j1 - j0], F32, raw_name(a, j0))
             rows = dy[a * K_PASS : (a + 1) * K_PASS, j0:j1]
             nc.sync.dma_start(out=tile[:], in_=rows.rearrange("(p t) j -> p t j", t=PACK))
-            for j in range(j0, j1, CHUNK):
+            for j in range(j0, j1, P):
                 raw[a, j] = (tile, j - j0)
 
         def load_scales(a, dram):
@@ -65,30 +58,29 @@ def tile_list_embg_mix_none_kernel(tc, dy, w8_words, w8_scales, w4_words, w4_sca
                     in_=dram[0, 4 * q : 4 * q + 4, :].bitcast(I32),
                 )
 
+        def load_w8():
+            nc.sync.dma_start(out=w8[:].bitcast(I32), in_=w8_words[0].rearrange("p n t -> p (n t)").bitcast(I32))
+
+        def load_w4():
+            nc.sync.dma_start(out=w4[:].bitcast(I32), in_=w4_words[0].bitcast(I32))
+
         def load_gains(j0, j1):
             nc.sync.dma_start(out=gains[:, j0:j1], in_=wgo[:, j0:j1])
 
-        def zero_on_vector(window, width):
-            cut = width // 2 - 1
-            for c0, c1 in ((0, cut), (cut, width)):
-                nc.vector.memset(window[:, c0:c1].bitcast(I32), 0)
+        def zero_on_vector(window, c0, c1):
+            cut = (c0 + c1) // 2 - 1
+            for a, b in ((c0, cut), (cut, c1)):
+                nc.vector.memset(window[:, a:b].bitcast(I32), 0)
 
-        def zero_on_both(window, vector_share):
-            zero_on_vector(window, vector_share)
-            nc.gpsimd.memset(window[:, vector_share:T].bitcast(I32), 0)
+        def zero_on_gpsimd(window, c0, c1):
+            nc.gpsimd.memset(window[:, c0:c1].bitcast(I32), 0)
 
         def interleave(engine_copy, rounded, a, j0, width):
             tile, c0 = raw[a, j0]
             engine_copy(
-                out=rounded.rearrange("p (c i) t -> p c t i", i=4),
+                out=rounded.rearrange("p (c i t) -> p c t i", i=4, t=PACK),
                 in_=tile[:, :, c0 : c0 + width].rearrange("p t (c i) -> p c t i", i=4),
             )
-
-        def new_rounded(name, on=None):
-            return sbuf([P, 2, CHUNK, PACK], BF16, name, on)
-
-        def flat(rounded):
-            return rounded.rearrange("p a j t -> p (a j t)")
 
         def new_codes(name, width):
             return sbuf([P, width], U32, "codes" + name), sbuf([P, width], U8, "scales" + name)
@@ -96,174 +88,138 @@ def tile_list_embg_mix_none_kernel(tc, dy, w8_words, w8_scales, w4_words, w4_sca
         def quantize(codes, scales, rounded):
             nc.vector.quantize_mx(out=codes.bitcast(E5M2), scales=scales, in_=rounded)
 
-        def multiply_chunk(c, codes, scales, bank_tag):
-            bank = psum.tile([P, N], F32, name="product%d" % c, tag=bank_tag)
-            weights = [w8[:].bitcast(E4M3), w4[:].bitcast(E2M1)]
-            for a in (LOW, HIGH):
-                cols = slice(a * CHUNK, (a + 1) * CHUNK)
-                nc.tensor.matmul_mx(
-                    out=bank[:],
-                    lhsT=codes[:, cols].bitcast(E5M2),
-                    lhsT_scale=scales[:, cols],
-                    rhs=weights[a],
-                    rhs_scale=w_scales[:, a * N : (a + 1) * N],
-                    start=a == LOW,
-                    stop=a == HIGH,
-                )
+        def one_pass(dst, a, b, codes, scales):
+            n0, n1 = b * P, (b + 1) * P
+            weights = w8[:, n0:n1].bitcast(E4M3) if a == LOW else w4[:, 2 * n0 : 2 * n1].bitcast(E2M1)
+            nc.tensor.matmul_mx(
+                out=dst,
+                lhsT=weights,
+                lhsT_scale=w_scales[:, a * N + n0 : a * N + n1],
+                rhs=codes.bitcast(E5M2),
+                rhs_scale=scales,
+                start=a == LOW,
+                stop=a == HIGH,
+            )
+
+        def multiply(name, bank_tag, groups, codes, scales, width):
+            bank = psum.tile([P, len(groups) * width], F32, name=name, tag=bank_tag)
+            for i, b in enumerate(groups):
+                for a in (LOW, HIGH):
+                    cols = slice(a * width, (a + 1) * width)
+                    one_pass(bank[:, i * width : (i + 1) * width], a, b, codes[:, cols], scales[:, cols])
             return bank
 
-        def new_squares(name, count, on=None):
-            return sbuf([P, count, P], F32, name, on)
-
-        def copy_out(bank, b0, b1, squares):
-            nc.scalar.copy(out=squares, in_=bank[:, b0 * P : b1 * P].rearrange("p (b c) -> p b c", c=P))
-            return [squares[:, i, :] for i in range(b1 - b0)]
-
-        def turn(name, by_token, b0, bank_tag):
-            bank = psum.tile([P, N], F32, name=name, tag=bank_tag)
-            for i, square in enumerate(by_token):
-                nc.tensor.transpose(bank[:, (b0 + i) * P : (b0 + i + 1) * P], square, identity[:])
-            return bank
+        def copy_out(bank, width, name, on=None):
+            values = sbuf([P, width], F32, name, on)
+            nc.scalar.copy(out=values[:], in_=bank[:])
+            return values
 
         def scatter(b, values, j0, j1):
             places = windows[b][:].indirect(offsets[:, j0 // LIST_ROWS : j1 // LIST_ROWS])
             nc.vector.tensor_tensor(places, values, gains[:, j0:j1], MULT)
 
-        def scatter_chunk(c, values, b0):
-            for i, square in enumerate(values):
-                scatter(b0 + i, square, c * CHUNK, (c + 1) * CHUNK)
-
-        make_identity(nc, identity[:])
-        zero_on_vector(windows[0], T)
-        zero_on_both(windows[1], VECTOR_ZEROES_1)
-
-        load_dy(LOW, 0, CHUNK)
-        load_scales(LOW, w8_scales)
-        load_dy(HIGH, 0, CHUNK)
-        nc.sync.dma_start(out=w8[:].bitcast(I32), in_=w8_words[0].rearrange("p n t -> p (n t)").bitcast(I32))
-        nc.sync.dma_start(out=w4[:].bitcast(I32), in_=w4_words[0].bitcast(I32))
-        load_scales(HIGH, w4_scales)
-        load_dy(LOW, CHUNK, 2 * CHUNK)
-        load_dy(HIGH, CHUNK, 2 * CHUNK)
-        nc.sync.dma_start(offsets[:], offs)
-        load_gains(0, 2 * CHUNK)
-        for c in (2, 3):
-            load_dy(LOW, c * CHUNK, (c + 1) * CHUNK)
-            load_dy(HIGH, c * CHUNK, (c + 1) * CHUNK)
-        load_dy(LOW, HALF, HALF + PIECE)
-        load_gains(2 * CHUNK, HALF)
-        load_dy(LOW, HALF + PIECE, J)
-        load_dy(HIGH, HALF, HALF + PIECE)
-        load_dy(HIGH, HALF + PIECE, J)
-        load_gains(HALF, J)
-
-        rounded0 = new_rounded("rounded0")
-        rounded1 = new_rounded("rounded1")
-        codes0, scales0 = new_codes("0", 2 * CHUNK)
-        codes1, scales1 = new_codes("1", 2 * CHUNK)
-        for a, engine_copy in ((LOW, nc.scalar.copy), (HIGH, nc.vector.tensor_copy)):
-            cols = slice(a * CHUNK, (a + 1) * CHUNK)
-            interleave(engine_copy, rounded0[:, a], a, 0, CHUNK)
-            quantize(codes0[:, cols], scales0[:, cols], flat(rounded0[:, a : a + 1]))
-        windows.append(sbuf([P, T], F32, "window2", "rounded0"))
-        zero_on_both(windows[2], VECTOR_ZEROES_2)
-        product = multiply_chunk(0, codes0, scales0, "bank_a")
-        by_token0 = new_squares("by_token0", GROUPS)
-        lead = copy_out(product, 0, 1, by_token0[:, 0:1, :])
-        others = copy_out(product, 1, GROUPS, by_token0[:, 1:GROUPS, :])
-        turned_lead = turn("lead0", lead, 0, "bank_b")
-        turned_others = turn("others0", others, 1, "bank_c")
-        values_lead = copy_out(turned_lead, 0, 1, new_squares("values00", 1)[:])
-        values_others = copy_out(turned_others, 1, GROUPS, new_squares("values01", GROUPS - 1)[:])
-
-        for a in (LOW, HIGH):
-            interleave(nc.vector.tensor_copy, rounded1[:, a], a, CHUNK, CHUNK)
-        for a in (LOW, HIGH):
-            cols = slice(a * CHUNK, (a + 1) * CHUNK)
-            quantize(codes1[:, cols], scales1[:, cols], flat(rounded1[:, a : a + 1]))
-        windows.append(sbuf([P, T], F32, "window3", "rounded1"))
-        nc.gpsimd.memset(windows[3][:].bitcast(I32), 0)
-        scatter_chunk(0, values_lead, 0)
-        scatter_chunk(0, values_others, 1)
-
-        rounded2 = new_rounded("rounded2", "by_token0")
-        interleave(nc.scalar.copy, rounded2[:, LOW], LOW, 2 * CHUNK, CHUNK)
-        product = multiply_chunk(1, codes1, scales1, "bank_a")
-        by_token1 = copy_out(product, 0, GROUPS, new_squares("by_token1", GROUPS, raw_name(LOW, 2 * CHUNK))[:])
-        turned_front = turn("front1", by_token1[0:2], 0, "bank_b")
-        turned_back = turn("back1", by_token1[2:GROUPS], 2, "bank_d")
-        interleave(nc.scalar.copy, rounded2[:, HIGH], HIGH, 2 * CHUNK, CHUNK)
-        rounded3 = new_rounded("rounded3", "codes1")
-        interleave(nc.scalar.copy, rounded3[:, LOW], LOW, 3 * CHUNK, CHUNK)
-        values_front = copy_out(turned_front, 0, 2, new_squares("values10", 2, raw_name(HIGH, 2 * CHUNK))[:])
-        codes2, scales2 = new_codes("2", 2 * CHUNK)
-        quantize(codes2[:], scales2[:], flat(rounded2[:]))
-        scatter_chunk(1, values_front, 0)
-        interleave(nc.scalar.copy, rounded3[:, HIGH], HIGH, 3 * CHUNK, CHUNK)
-        values_back = copy_out(turned_back, 2, GROUPS, new_squares("values12", 2, raw_name(HIGH, 3 * CHUNK))[:])
-        codes3, scales3 = new_codes("3", 2 * CHUNK)
-        quantize(codes3[:], scales3[:], flat(rounded3[:]))
-        scatter_chunk(1, values_back, 2)
-
-        late = sbuf([P, 2 * HALF * PACK], BF16, "late", "by_token0")
-
-        def late_column(a, j):
-            return (a * HALF + j) * PACK
-
-        def round_late(a, j0, width):
-            piece = late[:, late_column(a, j0) : late_column(a, j0 + width)]
-            interleave(nc.scalar.copy, piece.rearrange("p (j t) -> p j t", t=PACK), a, HALF + j0, width)
-
-        def squares_on_late(c0, count):
-            return late[:, c0 : c0 + 2 * P * count].bitcast(F32).rearrange("p (b c) -> p b c", c=P)
-
-        round_late(LOW, 0, CHUNK)
-        product = multiply_chunk(2, codes2, scales2, "bank_b")
-        lead = copy_out(product, 0, 1, squares_on_late(late_column(HIGH, 0) - P, 1))
-        others = copy_out(product, 1, GROUPS, squares_on_late(late_column(LOW, PIECE), GROUPS - 1))
-        turned_lead = turn("lead2", lead, 0, "bank_a")
-        turned_others = turn("others2", others, 1, "bank_c")
-        round_late(LOW, CHUNK, CHUNK)
-        values_lead = copy_out(turned_lead, 0, 1, new_squares("values20", 1)[:])
-        values_others = copy_out(turned_others, 1, GROUPS, new_squares("values21", GROUPS - 1)[:])
-        scatter_chunk(2, values_lead + values_others, 0)
-
-        round_late(LOW, PIECE, PIECE)
-        product = multiply_chunk(3, codes3, scales3, "bank_a")
-        lead = copy_out(product, 0, 1, squares_on_late(late_column(HIGH, PIECE) - P, 1))
-        others = copy_out(product, 1, GROUPS, new_squares("by_token3", GROUPS - 1)[:])
-        turned_lead = turn("lead3", lead, 0, "bank_b")
-        turned_others = turn("others3", others, 1, "bank_d")
-        round_late(HIGH, 0, CHUNK)
-        values_lead = copy_out(turned_lead, 0, 1, new_squares("values30", 1)[:])
-        scatter_chunk(3, values_lead, 0)
-        round_late(HIGH, CHUNK, CHUNK)
-        round_late(HIGH, PIECE, PIECE)
-        values_others = copy_out(turned_others, 1, GROUPS, new_squares("values31", GROUPS - 1, raw_name(HIGH, HALF))[:])
-        late_codes = []
-        for a, name in ((LOW, "low"), (HIGH, "high")):
-            codes, scales = new_codes(name, HALF)
-            quantize(codes[:], scales[:], late[:, late_column(a, 0) : late_column(a, HALF)])
-            late_codes.append((codes, scales))
-        scatter_chunk(3, values_others, 1)
-
-        for b in range(GROUPS):
-            n0, n1 = b * P, (b + 1) * P
-            product = psum.tile([P, HALF], F32, name="late_product%d" % b, tag="bank_late")
-            weights = [w8[:, n0:n1].bitcast(E4M3), w4[:, 2 * n0 : 2 * n1].bitcast(E2M1)]
-            for a in (LOW, HIGH):
-                codes, scales = late_codes[a]
-                nc.tensor.matmul_mx(
-                    out=product[:],
-                    lhsT=weights[a],
-                    lhsT_scale=w_scales[:, a * N + n0 : a * N + n1],
-                    rhs=codes[:].bitcast(E5M2),
-                    rhs_scale=scales[:],
-                    start=a == LOW,
-                    stop=a == HIGH,
-                )
-            values = sbuf([P, HALF], F32, "late_values%d" % b)
-            nc.scalar.copy(out=values[:], in_=product[:])
-            scatter(b, values[:], HALF, J)
+        def store(b):
             for c0, c1 in ((0, T // 2), (T // 2, T)) if b == GROUPS - 1 else ((0, T),):
-                nc.sync.dma_start(out=out[n0:n1, c0:c1], in_=windows[b][:, c0:c1])
+                nc.sync.dma_start(out=out[b * P : (b + 1) * P, c0:c1], in_=windows[b][:, c0:c1])
+
+        for b in range(3):
+            windows[b] = sbuf([P, T], F32, "window%d" % b)
+        for b in range(3):
+            nc.vector.memset(windows[b][:].bitcast(I32), 0)
+
+        load_dy(LOW, 0, 128)
+        load_scales(LOW, w8_scales)
+        load_dy(HIGH, 0, 128)
+        load_w8()
+        load_w4()
+        load_scales(HIGH, w4_scales)
+        nc.sync.dma_start(offsets[:], offs)
+        load_dy(LOW, 128, 256)
+        load_gains(0, 128)
+        load_dy(HIGH, 128, 256)
+        load_dy(LOW, 256, 512)
+        load_gains(128, 512)
+        load_dy(HIGH, 256, 512)
+        load_dy(LOW, 512, 768)
+        load_dy(HIGH, 512, 768)
+        load_dy(LOW, 768, J)
+        load_dy(HIGH, 768, J)
+        load_gains(512, J)
+
+        rounded0 = sbuf([P, 1024], BF16, "rounded0")
+        codes0, scales0 = new_codes("0", 256)
+        for a in (LOW, HIGH):
+            interleave(nc.scalar.copy, rounded0[:, a * 512 : (a + 1) * 512], a, 0, 128)
+        quantize(codes0[:], scales0[:], rounded0[:])
+        windows[3] = sbuf([P, T], F32, "window3", "rounded0")
+        nc.vector.memset(windows[3][:].bitcast(I32), 0)
+        p00 = multiply("p00", "bank0", [0], codes0, scales0, 128)
+        p01 = multiply("p01", "bank1", [1], codes0, scales0, 128)
+        p02 = multiply("p02", "bank2", [2, 3], codes0, scales0, 128)
+        scatter(0, copy_out(p00, 128, "v00")[:], 0, 128)
+        scatter(1, copy_out(p01, 128, "v01")[:], 0, 128)
+
+        rounded1 = sbuf([P, 1024], BF16, "rounded1")
+        codes1, scales1 = new_codes("1", 256)
+        for a in (LOW, HIGH):
+            interleave(nc.scalar.copy, rounded1[:, a * 512 : (a + 1) * 512], a, 128, 128)
+        v02 = copy_out(p02, 256, "v02", raw_name(HIGH, 128))
+        quantize(codes1[:], scales1[:], rounded1[:])
+        scatter(2, v02[:, 0:128], 0, 128)
+        scatter(3, v02[:, 128:256], 0, 128)
+        p10 = multiply("p10", "bank3", [0], codes1, scales1, 128)
+        p11 = multiply("p11", "bank4", [1], codes1, scales1, 128)
+        p12 = multiply("p12", "bank5", [2, 3], codes1, scales1, 128)
+
+        rounded2 = sbuf([P, 2048], BF16, "rounded2", "rounded1")
+        codes2, scales2 = new_codes("2", 512)
+        interleave(nc.scalar.copy, rounded2[:, 0:512], LOW, 256, 128)
+        scatter(0, copy_out(p10, 128, "v10")[:], 128, 256)
+        scatter(1, copy_out(p11, 128, "v11")[:], 128, 256)
+        interleave(nc.scalar.copy, rounded2[:, 512:1024], LOW, 384, 128)
+        quantize(codes2[:, 0:256], scales2[:, 0:256], rounded2[:, 0:1024])
+        interleave(nc.scalar.copy, rounded2[:, 1024:2048], HIGH, 256, 256)
+        v12 = copy_out(p12, 256, "v12", raw_name(HIGH, 256))
+        quantize(codes2[:, 256:512], scales2[:, 256:512], rounded2[:, 1024:2048])
+        scatter(2, v12[:, 0:128], 128, 256)
+        scatter(3, v12[:, 128:256], 128, 256)
+        p20 = multiply("p20", "bank6", [0], codes2, scales2, 256)
+        p21 = multiply("p21", "bank7", [1], codes2, scales2, 256)
+        p22 = multiply("p22", "bank0", [2, 3], codes2, scales2, 256)
+
+        rounded3 = sbuf([P, 2048], BF16, "rounded3", "rounded1")
+        codes3, scales3 = new_codes("3", 512)
+        interleave(nc.scalar.copy, rounded3[:, 0:512], LOW, 512, 128)
+        scatter(0, copy_out(p20, 256, "v20")[:], 256, 512)
+        scatter(1, copy_out(p21, 256, "v21")[:], 256, 512)
+        interleave(nc.scalar.copy, rounded3[:, 512:1024], LOW, 640, 128)
+        interleave(nc.scalar.copy, rounded3[:, 1024:2048], HIGH, 512, 256)
+        v22 = copy_out(p22, 512, "v22", raw_name(HIGH, 512))
+        quantize(codes3[:], scales3[:], rounded3[:])
+        scatter(2, v22[:, 0:256], 256, 512)
+        scatter(3, v22[:, 256:512], 256, 512)
+        p30 = multiply("p30", "bank1", [0, 1], codes3, scales3, 256)
+        last = [psum.tile([P, 512], F32, name="last%d" % b, tag="bank%d" % b) for b in (2, 3)]
+        for b in (2, 3):
+            for a in (LOW, HIGH):
+                one_pass(last[b - 2][:, 0:256], a, b, codes3[:, a * 256 : (a + 1) * 256], scales3[:, a * 256 : (a + 1) * 256])
+
+        rounded4 = sbuf([P, 2048], BF16, "rounded4")
+        codes4, scales4 = new_codes("4", 512)
+        interleave(nc.scalar.copy, rounded4[:, 0:512], LOW, 768, 128)
+        interleave(nc.scalar.copy, rounded4[:, 512:1024], LOW, 896, 128)
+        interleave(nc.scalar.copy, rounded4[:, 1024:2048], HIGH, 768, 256)
+        v30 = copy_out(p30, 512, "v30", raw_name(HIGH, 768))
+        quantize(codes4[:], scales4[:], rounded4[:])
+        scatter(0, v30[:, 0:256], 512, 768)
+        scatter(1, v30[:, 256:512], 512, 768)
+        p40 = multiply("p40", "bank4", [0, 1], codes4, scales4, 256)
+        v40 = copy_out(p40, 512, "v40")
+        for b in (0, 1):
+            scatter(b, v40[:, b * 256 : (b + 1) * 256], 768, J)
+            store(b)
+        for b in (2, 3):
+            for a in (LOW, HIGH):
+                one_pass(last[b - 2][:, 256:512], a, b, codes4[:, a * 256 : (a + 1) * 256], scales4[:, a * 256 : (a + 1) * 256])
+            scatter(b, copy_out(last[b - 2], 512, "v4%d" % b)[:], 512, J)
+            store(b)

@@ -101,11 +101,12 @@ def tile_list_embg_mix_none_kernel(tc, dy, w8_words, w8_scales, w4_words, w4_sca
                 stop=a == HIGH,
             )
 
-        def multiply(name, bank_tag, groups, codes, scales, width):
+        def multiply(name, bank_tag, groups, codes, scales, width, first=0, pitch=None):
             bank = psum.tile([P, len(groups) * width], F32, name=name, tag=bank_tag)
             for i, b in enumerate(groups):
                 for a in (LOW, HIGH):
-                    cols = slice(a * width, (a + 1) * width)
+                    c0 = a * (pitch or width) + first
+                    cols = slice(c0, c0 + width)
                     one_pass(bank[:, i * width : (i + 1) * width], a, b, codes[:, cols], scales[:, cols])
             return bank
 
@@ -124,62 +125,61 @@ def tile_list_embg_mix_none_kernel(tc, dy, w8_words, w8_scales, w4_words, w4_sca
 
         for b in range(3):
             windows[b] = sbuf([P, T], F32, "window%d" % b)
-        for b in range(3):
             nc.vector.memset(windows[b][:].bitcast(I32), 0)
 
         load_dy(LOW, 0, 128)
+        nc.sync.dma_start(offsets[:], offs)
         load_scales(LOW, w8_scales)
-        load_dy(HIGH, 0, 128)
+        load_dy(HIGH, 0, 256)
         load_w8()
         load_w4()
         load_scales(HIGH, w4_scales)
-        nc.sync.dma_start(offsets[:], offs)
+        load_gains(0, 256)
         load_dy(LOW, 128, 256)
-        load_gains(0, 128)
-        load_dy(HIGH, 128, 256)
         load_dy(LOW, 256, 512)
-        load_gains(128, 512)
         load_dy(HIGH, 256, 512)
+        load_gains(256, 512)
         load_dy(LOW, 512, 768)
         load_dy(HIGH, 512, 768)
         load_dy(LOW, 768, J)
         load_dy(HIGH, 768, J)
         load_gains(512, J)
 
-        rounded0 = sbuf([P, 1024], BF16, "rounded0")
-        codes0, scales0 = new_codes("0", 256)
-        for a in (LOW, HIGH):
-            interleave(nc.scalar.copy, rounded0[:, a * 512 : (a + 1) * 512], a, 0, 128)
-        quantize(codes0[:], scales0[:], rounded0[:])
-        windows[3] = sbuf([P, T], F32, "window3", "rounded0")
+        codes0, scales0 = new_codes("0", 512)
+
+        def prepare(a, c):
+            c0 = 256 * a + 128 * c
+            rounded = sbuf([P, 512], BF16, "rounded%d%d" % (a, c))
+            interleave(nc.scalar.copy, rounded[:], a, 128 * c, 128)
+            quantize(codes0[:, c0 : c0 + 128], scales0[:, c0 : c0 + 128], rounded[:])
+
+        prepare(LOW, 0)
+        windows[3] = sbuf([P, T], F32, "window3", "rounded00")
         nc.vector.memset(windows[3][:].bitcast(I32), 0)
-        p00 = multiply("p00", "bank0", [0], codes0, scales0, 128)
-        p01 = multiply("p01", "bank1", [1], codes0, scales0, 128)
-        p02 = multiply("p02", "bank2", [2, 3], codes0, scales0, 128)
+        prepare(HIGH, 0)
+        prepare(HIGH, 1)
+        p00 = multiply("p00", "bank0", [0], codes0, scales0, 128, 0, 256)
+        p01 = multiply("p01", "bank1", [1], codes0, scales0, 128, 0, 256)
+        p02 = multiply("p02", "bank2", [2, 3], codes0, scales0, 128, 0, 256)
         scatter(0, copy_out(p00, 128, "v00")[:], 0, 128)
         scatter(1, copy_out(p01, 128, "v01")[:], 0, 128)
-
-        rounded1 = sbuf([P, 1024], BF16, "rounded1")
-        codes1, scales1 = new_codes("1", 256)
-        for a in (LOW, HIGH):
-            interleave(nc.scalar.copy, rounded1[:, a * 512 : (a + 1) * 512], a, 128, 128)
-        v02 = copy_out(p02, 256, "v02", raw_name(HIGH, 128))
-        quantize(codes1[:], scales1[:], rounded1[:])
+        prepare(LOW, 1)
+        v02 = copy_out(p02, 256, "v02", raw_name(LOW, 128))
         scatter(2, v02[:, 0:128], 0, 128)
         scatter(3, v02[:, 128:256], 0, 128)
-        p10 = multiply("p10", "bank3", [0], codes1, scales1, 128)
-        p11 = multiply("p11", "bank4", [1], codes1, scales1, 128)
-        p12 = multiply("p12", "bank5", [2, 3], codes1, scales1, 128)
+        p10 = multiply("p10", "bank0", [0], codes0, scales0, 128, 128, 256)
+        p11 = multiply("p11", "bank1", [1], codes0, scales0, 128, 128, 256)
+        p12 = multiply("p12", "bank3", [2, 3], codes0, scales0, 128, 128, 256)
 
-        rounded2 = sbuf([P, 2048], BF16, "rounded2", "rounded1")
+        rounded2 = sbuf([P, 2048], BF16, "rounded2", "rounded01")
         codes2, scales2 = new_codes("2", 512)
         interleave(nc.scalar.copy, rounded2[:, 0:512], LOW, 256, 128)
         scatter(0, copy_out(p10, 128, "v10")[:], 128, 256)
         scatter(1, copy_out(p11, 128, "v11")[:], 128, 256)
         interleave(nc.scalar.copy, rounded2[:, 512:1024], LOW, 384, 128)
-        quantize(codes2[:, 0:256], scales2[:, 0:256], rounded2[:, 0:1024])
         interleave(nc.scalar.copy, rounded2[:, 1024:2048], HIGH, 256, 256)
         v12 = copy_out(p12, 256, "v12", raw_name(HIGH, 256))
+        quantize(codes2[:, 0:256], scales2[:, 0:256], rounded2[:, 0:1024])
         quantize(codes2[:, 256:512], scales2[:, 256:512], rounded2[:, 1024:2048])
         scatter(2, v12[:, 0:128], 128, 256)
         scatter(3, v12[:, 128:256], 128, 256)
@@ -187,7 +187,7 @@ def tile_list_embg_mix_none_kernel(tc, dy, w8_words, w8_scales, w4_words, w4_sca
         p21 = multiply("p21", "bank7", [1], codes2, scales2, 256)
         p22 = multiply("p22", "bank0", [2, 3], codes2, scales2, 256)
 
-        rounded3 = sbuf([P, 2048], BF16, "rounded3", "rounded1")
+        rounded3 = sbuf([P, 2048], BF16, "rounded3", "rounded01")
         codes3, scales3 = new_codes("3", 512)
         interleave(nc.scalar.copy, rounded3[:, 0:512], LOW, 512, 128)
         scatter(0, copy_out(p20, 256, "v20")[:], 256, 512)

@@ -44,10 +44,10 @@ def tile_list_embg_mix_none_kernel(tc, dy, w8_words, w8_scales, w4_words, w4_sca
         def raw_name(a, j0):
             return "raw%d_%d" % (a, j0)
 
-        def load_dy(a, j0, j1):
+        def load_dy(a, j0, j1, queue=nc.sync):
             tile = sbuf([P, PACK, j1 - j0], F32, raw_name(a, j0))
             rows = dy[a * K_PASS : (a + 1) * K_PASS, j0:j1]
-            nc.sync.dma_start(out=tile[:], in_=rows.rearrange("(p t) j -> p t j", t=PACK))
+            queue.dma_start(out=tile[:], in_=rows.rearrange("(p t) j -> p t j", t=PACK))
             for j in range(j0, j1, P):
                 raw[a, j] = (tile, j - j0)
 
@@ -110,9 +110,9 @@ def tile_list_embg_mix_none_kernel(tc, dy, w8_words, w8_scales, w4_words, w4_sca
                     one_pass(bank[:, i * width : (i + 1) * width], a, b, codes[:, cols], scales[:, cols])
             return bank
 
-        def copy_out(bank, width, name, on=None):
+        def copy_out(bank, width, name, on=None, engine_copy=nc.scalar.copy):
             values = sbuf([P, width], F32, name, on)
-            nc.scalar.copy(out=values[:], in_=bank[:])
+            engine_copy(out=values[:], in_=bank[:])
             return values
 
         def scatter(b, values, j0, j1):
@@ -154,10 +154,12 @@ def tile_list_embg_mix_none_kernel(tc, dy, w8_words, w8_scales, w4_words, w4_sca
             quantize(codes0[:, c0 : c0 + 128], scales0[:, c0 : c0 + 128], rounded[:])
 
         prepare(LOW, 0)
-        windows[3] = sbuf([P, T], F32, "window3", "rounded00")
-        nc.vector.memset(windows[3][:].bitcast(I32), 0)
         prepare(HIGH, 0)
         prepare(HIGH, 1)
+        windows[3] = sbuf([P, T], F32, "window3", "rounded11")
+        nc.vector.memset(windows[3][:, 0:447].bitcast(I32), 0)
+        nc.gpsimd.memset(windows[3][:, 448:T].bitcast(I32), 0)
+        nc.vector.memset(windows[3][:, 447:448].bitcast(I32), 0)
         p00 = multiply("p00", "bank0", [0], codes0, scales0, 128, 0, 256)
         p01 = multiply("p01", "bank1", [1], codes0, scales0, 128, 0, 256)
         p02 = multiply("p02", "bank2", [2, 3], codes0, scales0, 128, 0, 256)

@@ -88,7 +88,7 @@ def tile_list_embg_mix_none_kernel(tc, dy, w8_words, w8_scales, w4_words, w4_sca
         def quantize(codes, scales, rounded):
             nc.vector.quantize_mx(out=codes.bitcast(E5M2), scales=scales, in_=rounded)
 
-        def one_pass(dst, a, b, codes, scales):
+        def one_pass(dst, a, b, codes, scales, first=LOW):
             n0, n1 = b * P, (b + 1) * P
             weights = w8[:, n0:n1].bitcast(E4M3) if a == LOW else w4[:, 2 * n0 : 2 * n1].bitcast(E2M1)
             nc.tensor.matmul_mx(
@@ -97,18 +97,21 @@ def tile_list_embg_mix_none_kernel(tc, dy, w8_words, w8_scales, w4_words, w4_sca
                 lhsT_scale=w_scales[:, a * N + n0 : a * N + n1],
                 rhs=codes.bitcast(E5M2),
                 rhs_scale=scales,
-                start=a == LOW,
-                stop=a == HIGH,
+                start=a == first,
+                stop=a != first,
             )
 
-        def multiply(name, bank_tag, groups, codes, scales, width, first=0, pitch=None):
+        def multiply(name, bank_tag, groups, operands, first=LOW):
+            width = operands[LOW][0].shape[1]
             bank = psum.tile([P, len(groups) * width], F32, name=name, tag=bank_tag)
             for i, b in enumerate(groups):
-                for a in (LOW, HIGH):
-                    c0 = a * (pitch or width) + first
-                    cols = slice(c0, c0 + width)
-                    one_pass(bank[:, i * width : (i + 1) * width], a, b, codes[:, cols], scales[:, cols])
+                for a in (first, 1 - first):
+                    one_pass(bank[:, i * width : (i + 1) * width], a, b, *operands[a], first)
             return bank
+
+        def halves(codes, scales):
+            width = codes.shape[1] // 2
+            return [(codes[:, a * width : (a + 1) * width], scales[:, a * width : (a + 1) * width]) for a in (LOW, HIGH)]
 
         def copy_out(bank, width, name, on=None, engine_copy=nc.scalar.copy):
             values = sbuf([P, width], F32, name, on)
@@ -128,55 +131,57 @@ def tile_list_embg_mix_none_kernel(tc, dy, w8_words, w8_scales, w4_words, w4_sca
             nc.vector.memset(windows[b][:].bitcast(I32), 0)
 
         load_dy(LOW, 0, 128)
-        nc.sync.dma_start(offsets[:], offs)
+        load_gains(0, 128)
         load_scales(LOW, w8_scales)
         load_dy(HIGH, 0, 256)
         load_w8()
         load_w4()
         load_scales(HIGH, w4_scales)
-        load_gains(0, 256)
         load_dy(LOW, 128, 256)
-        load_dy(LOW, 256, 512)
+        nc.sync.dma_start(offsets[:], offs)
+        load_dy(LOW, 256, 384)
+        load_gains(128, 512)
+        load_dy(LOW, 384, 512)
         load_dy(HIGH, 256, 512)
-        load_gains(256, 512)
         load_dy(LOW, 512, 768)
         load_dy(HIGH, 512, 768)
         load_dy(LOW, 768, J)
         load_dy(HIGH, 768, J)
         load_gains(512, J)
 
-        codes0, scales0 = new_codes("0", 512)
 
-        def prepare(a, c):
-            c0 = 256 * a + 128 * c
-            rounded = sbuf([P, 512], BF16, "rounded%d%d" % (a, c))
+        def prepare(a, c, on=None):
+            rounded = sbuf([P, 512], BF16, "rounded%d%d" % (a, c), on)
+            codes = sbuf([P, 128], U32, "codes%d%d" % (a, c))
+            scales = sbuf([P, 128], U8, "scales%d%d" % (a, c))
             interleave(nc.scalar.copy, rounded[:], a, 128 * c, 128)
-            quantize(codes0[:, c0 : c0 + 128], scales0[:, c0 : c0 + 128], rounded[:])
+            quantize(codes[:], scales[:], rounded[:])
+            return codes[:], scales[:]
 
-        prepare(LOW, 0)
-        prepare(HIGH, 0)
-        prepare(HIGH, 1)
+        low0 = prepare(LOW, 0)
+        chunk0 = [low0, prepare(HIGH, 0)]
+        high1 = prepare(HIGH, 1)
         windows[3] = sbuf([P, T], F32, "window3", "rounded11")
         nc.vector.memset(windows[3][:, 0:447].bitcast(I32), 0)
         nc.gpsimd.memset(windows[3][:, 448:T].bitcast(I32), 0)
         nc.vector.memset(windows[3][:, 447:448].bitcast(I32), 0)
-        p00 = multiply("p00", "bank0", [0], codes0, scales0, 128, 0, 256)
-        p01 = multiply("p01", "bank1", [1], codes0, scales0, 128, 0, 256)
-        p02 = multiply("p02", "bank2", [2, 3], codes0, scales0, 128, 0, 256)
+        p00 = multiply("p00", "bank0", [0], chunk0)
+        p01 = multiply("p01", "bank1", [1], chunk0)
+        p02 = multiply("p02", "bank2", [2, 3], chunk0)
         scatter(0, copy_out(p00, 128, "v00")[:], 0, 128)
         scatter(1, copy_out(p01, 128, "v01")[:], 0, 128)
-        prepare(LOW, 1)
+        chunk1 = [prepare(LOW, 1, "codes10"), high1]
         v02 = copy_out(p02, 256, "v02", raw_name(LOW, 128))
         scatter(2, v02[:, 0:128], 0, 128)
         scatter(3, v02[:, 128:256], 0, 128)
-        p10 = multiply("p10", "bank0", [0], codes0, scales0, 128, 128, 256)
-        p11 = multiply("p11", "bank1", [1], codes0, scales0, 128, 128, 256)
-        p12 = multiply("p12", "bank3", [2, 3], codes0, scales0, 128, 128, 256)
+        p10 = multiply("p10", "bank0", [0], chunk1)
+        p11 = multiply("p11", "bank1", [1], chunk1)
+        p12 = multiply("p12", "bank3", [2, 3], chunk1)
 
-        rounded2 = sbuf([P, 2048], BF16, "rounded2", "rounded01")
+        rounded2 = sbuf([P, 2048], BF16, "rounded2", "codes10")
         codes2, scales2 = new_codes("2", 512)
         interleave(nc.scalar.copy, rounded2[:, 0:512], LOW, 256, 128)
-        scatter(0, copy_out(p10, 128, "v10")[:], 128, 256)
+        scatter(0, copy_out(p10, 128, "v10", raw_name(LOW, 256))[:], 128, 256)
         scatter(1, copy_out(p11, 128, "v11")[:], 128, 256)
         interleave(nc.scalar.copy, rounded2[:, 512:1024], LOW, 384, 128)
         interleave(nc.scalar.copy, rounded2[:, 1024:2048], HIGH, 256, 256)
@@ -185,11 +190,11 @@ def tile_list_embg_mix_none_kernel(tc, dy, w8_words, w8_scales, w4_words, w4_sca
         quantize(codes2[:, 256:512], scales2[:, 256:512], rounded2[:, 1024:2048])
         scatter(2, v12[:, 0:128], 128, 256)
         scatter(3, v12[:, 128:256], 128, 256)
-        p20 = multiply("p20", "bank6", [0], codes2, scales2, 256)
-        p21 = multiply("p21", "bank7", [1], codes2, scales2, 256)
-        p22 = multiply("p22", "bank0", [2, 3], codes2, scales2, 256)
+        p20 = multiply("p20", "bank6", [0], halves(codes2, scales2))
+        p21 = multiply("p21", "bank7", [1], halves(codes2, scales2))
+        p22 = multiply("p22", "bank0", [2, 3], halves(codes2, scales2))
 
-        rounded3 = sbuf([P, 2048], BF16, "rounded3", "rounded01")
+        rounded3 = sbuf([P, 2048], BF16, "rounded3", "codes10")
         codes3, scales3 = new_codes("3", 512)
         interleave(nc.scalar.copy, rounded3[:, 0:512], LOW, 512, 128)
         scatter(0, copy_out(p20, 256, "v20")[:], 256, 512)
@@ -200,7 +205,7 @@ def tile_list_embg_mix_none_kernel(tc, dy, w8_words, w8_scales, w4_words, w4_sca
         quantize(codes3[:], scales3[:], rounded3[:])
         scatter(2, v22[:, 0:256], 256, 512)
         scatter(3, v22[:, 256:512], 256, 512)
-        p30 = multiply("p30", "bank1", [0, 1], codes3, scales3, 256)
+        p30 = multiply("p30", "bank1", [0, 1], halves(codes3, scales3))
         last = [psum.tile([P, 512], F32, name="last%d" % b, tag="bank%d" % b) for b in (2, 3)]
         for b in (2, 3):
             for a in (LOW, HIGH):
@@ -215,7 +220,7 @@ def tile_list_embg_mix_none_kernel(tc, dy, w8_words, w8_scales, w4_words, w4_sca
         quantize(codes4[:], scales4[:], rounded4[:])
         scatter(0, v30[:, 0:256], 512, 768)
         scatter(1, v30[:, 256:512], 512, 768)
-        p40 = multiply("p40", "bank4", [0, 1], codes4, scales4, 256)
+        p40 = multiply("p40", "bank4", [0, 1], halves(codes4, scales4))
         v40 = copy_out(p40, 512, "v40")
         for b in (0, 1):
             scatter(b, v40[:, b * 256 : (b + 1) * 256], 768, J)

@@ -150,16 +150,16 @@ def tile_list_embg_mix_none_kernel(tc, dy, w8_words, w8_scales, w4_words, w4_sca
         load_gains(512, J)
 
 
-        def prepare(a, c, on=None):
+        def prepare(a, c, on=None, engine_copy=nc.scalar.copy):
             rounded = sbuf([P, 512], BF16, "rounded%d%d" % (a, c), on)
             codes = sbuf([P, 128], U32, "codes%d%d" % (a, c))
             scales = sbuf([P, 128], U8, "scales%d%d" % (a, c))
-            interleave(nc.scalar.copy, rounded[:], a, 128 * c, 128)
+            interleave(engine_copy, rounded[:], a, 128 * c, 128)
             quantize(codes[:], scales[:], rounded[:])
             return codes[:], scales[:]
 
         low0 = prepare(LOW, 0)
-        chunk0 = [low0, prepare(HIGH, 0)]
+        chunk0 = [low0, prepare(HIGH, 0, None, nc.vector.tensor_copy)]
         high1 = prepare(HIGH, 1)
         windows[3] = sbuf([P, T], F32, "window3", "rounded11")
         nc.vector.memset(windows[3][:, 0:447].bitcast(I32), 0)

@@ -22,6 +22,10 @@ K_PASS = P * PACK
 GROUPS = N // P
 LIST_ROWS = 16
 LOW, HIGH = 0, 1
+NARROW = 128
+WIDE = 256
+START = [0, NARROW, 2 * NARROW, 2 * NARROW + WIDE, 2 * NARROW + 2 * WIDE, J]
+VECTOR_ZEROES_3 = 448
 
 
 def tile_list_embg_mix_none_kernel(tc, dy, w8_words, w8_scales, w4_words, w4_scales, wgo, offs, out):
@@ -38,17 +42,17 @@ def tile_list_embg_mix_none_kernel(tc, dy, w8_words, w8_scales, w4_words, w4_sca
         w8 = sbuf([P, N], U32, "w8")
         w4 = sbuf([P, 2 * N], U8, "w4")
         gains = sbuf([P, J], F32, "gains")
-        windows = {}
+        windows = []
         raw = {}
 
         def raw_name(a, j0):
             return "raw%d_%d" % (a, j0)
 
-        def load_dy(a, j0, j1, queue=nc.sync):
+        def load_dy(a, j0, j1):
             tile = sbuf([P, PACK, j1 - j0], F32, raw_name(a, j0))
             rows = dy[a * K_PASS : (a + 1) * K_PASS, j0:j1]
-            queue.dma_start(out=tile[:], in_=rows.rearrange("(p t) j -> p t j", t=PACK))
-            for j in range(j0, j1, P):
+            nc.sync.dma_start(out=tile[:], in_=rows.rearrange("(p t) j -> p t j", t=PACK))
+            for j in range(j0, j1, NARROW):
                 raw[a, j] = (tile, j - j0)
 
         def load_scales(a, dram):
@@ -58,22 +62,8 @@ def tile_list_embg_mix_none_kernel(tc, dy, w8_words, w8_scales, w4_words, w4_sca
                     in_=dram[0, 4 * q : 4 * q + 4, :].bitcast(I32),
                 )
 
-        def load_w8():
-            nc.sync.dma_start(out=w8[:].bitcast(I32), in_=w8_words[0].rearrange("p n t -> p (n t)").bitcast(I32))
-
-        def load_w4():
-            nc.sync.dma_start(out=w4[:].bitcast(I32), in_=w4_words[0].bitcast(I32))
-
         def load_gains(j0, j1):
             nc.sync.dma_start(out=gains[:, j0:j1], in_=wgo[:, j0:j1])
-
-        def zero_on_vector(window, c0, c1):
-            cut = (c0 + c1) // 2 - 1
-            for a, b in ((c0, cut), (cut, c1)):
-                nc.vector.memset(window[:, a:b].bitcast(I32), 0)
-
-        def zero_on_gpsimd(window, c0, c1):
-            nc.gpsimd.memset(window[:, c0:c1].bitcast(I32), 0)
 
         def interleave(engine_copy, rounded, a, j0, width):
             tile, c0 = raw[a, j0]
@@ -82,151 +72,156 @@ def tile_list_embg_mix_none_kernel(tc, dy, w8_words, w8_scales, w4_words, w4_sca
                 in_=tile[:, :, c0 : c0 + width].rearrange("p t (c i) -> p c t i", i=4),
             )
 
-        def new_codes(name, width):
-            return sbuf([P, width], U32, "codes" + name), sbuf([P, width], U8, "scales" + name)
-
         def quantize(codes, scales, rounded):
             nc.vector.quantize_mx(out=codes.bitcast(E5M2), scales=scales, in_=rounded)
 
-        def one_pass(dst, a, b, codes, scales, first=LOW):
+        def prepare_narrow(a, c, engine_copy, on=None):
+            rounded = sbuf([P, NARROW * PACK], BF16, "rounded%d%d" % (a, c), on)
+            codes = sbuf([P, NARROW], U32, "codes%d%d" % (a, c))
+            scales = sbuf([P, NARROW], U8, "scales%d%d" % (a, c))
+            interleave(engine_copy, rounded[:], a, START[c], NARROW)
+            quantize(codes[:], scales[:], rounded[:])
+            return codes[:], scales[:]
+
+        def new_wide(c, on=None):
+            rounded = sbuf([P, 2 * WIDE * PACK], BF16, "rounded%d" % c, on)
+            return rounded, sbuf([P, 2 * WIDE], U32, "codes%d" % c), sbuf([P, 2 * WIDE], U8, "scales%d" % c)
+
+        def round_wide(rounded, c, a, i0, i1):
+            piece = rounded[:, (a * WIDE + i0) * PACK : (a * WIDE + i1) * PACK]
+            interleave(nc.scalar.copy, piece, a, START[c] + i0, i1 - i0)
+
+        def by_pass(codes, scales):
+            return [(codes[:, a * WIDE : (a + 1) * WIDE], scales[:, a * WIDE : (a + 1) * WIDE]) for a in (LOW, HIGH)]
+
+        def both_passes(product, b, operands):
             n0, n1 = b * P, (b + 1) * P
-            weights = w8[:, n0:n1].bitcast(E4M3) if a == LOW else w4[:, 2 * n0 : 2 * n1].bitcast(E2M1)
-            nc.tensor.matmul_mx(
-                out=dst,
-                lhsT=weights,
-                lhsT_scale=w_scales[:, a * N + n0 : a * N + n1],
-                rhs=codes.bitcast(E5M2),
-                rhs_scale=scales,
-                start=a == first,
-                stop=a != first,
-            )
+            weights = [w8[:, n0:n1].bitcast(E4M3), w4[:, 2 * n0 : 2 * n1].bitcast(E2M1)]
+            for a in (LOW, HIGH):
+                codes, scales = operands[a]
+                nc.tensor.matmul_mx(
+                    out=product,
+                    lhsT=weights[a],
+                    lhsT_scale=w_scales[:, a * N + n0 : a * N + n1],
+                    rhs=codes.bitcast(E5M2),
+                    rhs_scale=scales,
+                    start=a == LOW,
+                    stop=a == HIGH,
+                )
 
-        def multiply(name, bank_tag, groups, operands, first=LOW):
-            width = operands[LOW][0].shape[1]
-            bank = psum.tile([P, len(groups) * width], F32, name=name, tag=bank_tag)
+        def multiply(c, groups, operands, bank):
+            width = START[c + 1] - START[c]
+            products = psum.tile([P, len(groups) * width], F32, name="product%d%d" % (c, groups[0]), tag="bank%d" % bank)
             for i, b in enumerate(groups):
-                for a in (first, 1 - first):
-                    one_pass(bank[:, i * width : (i + 1) * width], a, b, *operands[a], first)
-            return bank
+                both_passes(products[:, i * width : (i + 1) * width], b, operands)
+            return products
 
-        def halves(codes, scales):
-            width = codes.shape[1] // 2
-            return [(codes[:, a * width : (a + 1) * width], scales[:, a * width : (a + 1) * width]) for a in (LOW, HIGH)]
-
-        def copy_out(bank, width, name, on=None, engine_copy=nc.scalar.copy):
-            values = sbuf([P, width], F32, name, on)
-            engine_copy(out=values[:], in_=bank[:])
+        def copy_out(products, name, on=None):
+            values = sbuf([P, products.shape[1]], F32, name, on)
+            nc.scalar.copy(out=values[:], in_=products[:])
             return values
 
         def scatter(b, values, j0, j1):
             places = windows[b][:].indirect(offsets[:, j0 // LIST_ROWS : j1 // LIST_ROWS])
             nc.vector.tensor_tensor(places, values, gains[:, j0:j1], MULT)
 
+        def scatter_chunk(c, groups, values):
+            width = START[c + 1] - START[c]
+            for i, b in enumerate(groups):
+                scatter(b, values[:, i * width : (i + 1) * width], START[c], START[c + 1])
+
         def store(b):
             for c0, c1 in ((0, T // 2), (T // 2, T)) if b == GROUPS - 1 else ((0, T),):
                 nc.sync.dma_start(out=out[b * P : (b + 1) * P, c0:c1], in_=windows[b][:, c0:c1])
 
-        for b in range(3):
-            windows[b] = sbuf([P, T], F32, "window%d" % b)
+        for b in range(GROUPS - 1):
+            windows.append(sbuf([P, T], F32, "window%d" % b))
             nc.vector.memset(windows[b][:].bitcast(I32), 0)
 
-        load_dy(LOW, 0, 128)
-        load_gains(0, 128)
+        load_dy(LOW, START[0], START[1])
+        load_gains(START[0], START[1])
         load_scales(LOW, w8_scales)
-        load_dy(HIGH, 0, 256)
-        load_w8()
-        load_w4()
+        load_dy(HIGH, START[0], START[2])
+        nc.sync.dma_start(out=w8[:].bitcast(I32), in_=w8_words[0].rearrange("p n t -> p (n t)").bitcast(I32))
+        nc.sync.dma_start(out=w4[:].bitcast(I32), in_=w4_words[0].bitcast(I32))
         load_scales(HIGH, w4_scales)
-        load_dy(LOW, 128, 256)
+        load_dy(LOW, START[1], START[2])
         nc.sync.dma_start(offsets[:], offs)
-        load_dy(LOW, 256, 384)
-        load_gains(128, 512)
-        load_dy(LOW, 384, 512)
-        load_dy(HIGH, 256, 512)
-        load_dy(LOW, 512, 768)
-        load_dy(HIGH, 512, 768)
-        load_dy(LOW, 768, J)
-        load_dy(HIGH, 768, J)
-        load_gains(512, J)
+        load_dy(LOW, START[2], START[2] + NARROW)
+        load_gains(START[1], START[2])
+        load_dy(LOW, START[2] + NARROW, START[3])
+        load_dy(HIGH, START[2], START[3])
+        load_dy(LOW, START[3], START[4])
+        load_gains(START[2], START[3])
+        load_dy(HIGH, START[3], START[4])
+        load_dy(LOW, START[4], J)
+        load_dy(HIGH, START[4], J)
+        load_gains(START[3], J)
 
+        low0 = prepare_narrow(LOW, 0, nc.scalar.copy)
+        chunk0 = [low0, prepare_narrow(HIGH, 0, nc.vector.tensor_copy)]
+        high1 = prepare_narrow(HIGH, 1, nc.scalar.copy)
+        windows.append(sbuf([P, T], F32, "window3", "rounded11"))
+        nc.vector.memset(windows[3][:, 0 : VECTOR_ZEROES_3 - 1].bitcast(I32), 0)
+        nc.gpsimd.memset(windows[3][:, VECTOR_ZEROES_3:T].bitcast(I32), 0)
+        nc.vector.memset(windows[3][:, VECTOR_ZEROES_3 - 1 : VECTOR_ZEROES_3].bitcast(I32), 0)
+        first = multiply(0, [0], chunk0, 0)
+        second = multiply(0, [1], chunk0, 1)
+        others = multiply(0, [2, 3], chunk0, 2)
+        scatter_chunk(0, [0], copy_out(first, "values00"))
+        scatter_chunk(0, [1], copy_out(second, "values01"))
 
-        def prepare(a, c, on=None, engine_copy=nc.scalar.copy):
-            rounded = sbuf([P, 512], BF16, "rounded%d%d" % (a, c), on)
-            codes = sbuf([P, 128], U32, "codes%d%d" % (a, c))
-            scales = sbuf([P, 128], U8, "scales%d%d" % (a, c))
-            interleave(engine_copy, rounded[:], a, 128 * c, 128)
-            quantize(codes[:], scales[:], rounded[:])
-            return codes[:], scales[:]
+        chunk1 = [prepare_narrow(LOW, 1, nc.scalar.copy, "codes10"), high1]
+        scatter_chunk(0, [2, 3], copy_out(others, "values02", raw_name(LOW, START[1])))
+        first = multiply(1, [0], chunk1, 0)
+        second = multiply(1, [1], chunk1, 1)
+        others = multiply(1, [2, 3], chunk1, 3)
 
-        low0 = prepare(LOW, 0)
-        chunk0 = [low0, prepare(HIGH, 0, None, nc.vector.tensor_copy)]
-        high1 = prepare(HIGH, 1)
-        windows[3] = sbuf([P, T], F32, "window3", "rounded11")
-        nc.vector.memset(windows[3][:, 0:447].bitcast(I32), 0)
-        nc.gpsimd.memset(windows[3][:, 448:T].bitcast(I32), 0)
-        nc.vector.memset(windows[3][:, 447:448].bitcast(I32), 0)
-        p00 = multiply("p00", "bank0", [0], chunk0)
-        p01 = multiply("p01", "bank1", [1], chunk0)
-        p02 = multiply("p02", "bank2", [2, 3], chunk0)
-        scatter(0, copy_out(p00, 128, "v00")[:], 0, 128)
-        scatter(1, copy_out(p01, 128, "v01")[:], 0, 128)
-        chunk1 = [prepare(LOW, 1, "codes10"), high1]
-        v02 = copy_out(p02, 256, "v02", raw_name(LOW, 128))
-        scatter(2, v02[:, 0:128], 0, 128)
-        scatter(3, v02[:, 128:256], 0, 128)
-        p10 = multiply("p10", "bank0", [0], chunk1)
-        p11 = multiply("p11", "bank1", [1], chunk1)
-        p12 = multiply("p12", "bank3", [2, 3], chunk1)
+        rounded, codes, scales = new_wide(2, "codes10")
+        round_wide(rounded, 2, LOW, 0, NARROW)
+        scatter_chunk(1, [0], copy_out(first, "values10", raw_name(LOW, START[2])))
+        scatter_chunk(1, [1], copy_out(second, "values11"))
+        round_wide(rounded, 2, LOW, NARROW, WIDE)
+        round_wide(rounded, 2, HIGH, 0, WIDE)
+        values = copy_out(others, "values12", raw_name(HIGH, START[2]))
+        chunk2 = by_pass(codes, scales)
+        for a in (LOW, HIGH):
+            quantize(*chunk2[a], rounded[:, a * WIDE * PACK : (a + 1) * WIDE * PACK])
+        scatter_chunk(1, [2, 3], values)
+        first = multiply(2, [0], chunk2, 6)
+        second = multiply(2, [1], chunk2, 7)
+        others = multiply(2, [2, 3], chunk2, 0)
 
-        rounded2 = sbuf([P, 2048], BF16, "rounded2", "codes10")
-        codes2, scales2 = new_codes("2", 512)
-        interleave(nc.scalar.copy, rounded2[:, 0:512], LOW, 256, 128)
-        scatter(0, copy_out(p10, 128, "v10", raw_name(LOW, 256))[:], 128, 256)
-        scatter(1, copy_out(p11, 128, "v11")[:], 128, 256)
-        interleave(nc.scalar.copy, rounded2[:, 512:1024], LOW, 384, 128)
-        interleave(nc.scalar.copy, rounded2[:, 1024:2048], HIGH, 256, 256)
-        v12 = copy_out(p12, 256, "v12", raw_name(HIGH, 256))
-        quantize(codes2[:, 0:256], scales2[:, 0:256], rounded2[:, 0:1024])
-        quantize(codes2[:, 256:512], scales2[:, 256:512], rounded2[:, 1024:2048])
-        scatter(2, v12[:, 0:128], 128, 256)
-        scatter(3, v12[:, 128:256], 128, 256)
-        p20 = multiply("p20", "bank6", [0], halves(codes2, scales2))
-        p21 = multiply("p21", "bank7", [1], halves(codes2, scales2))
-        p22 = multiply("p22", "bank0", [2, 3], halves(codes2, scales2))
-
-        rounded3 = sbuf([P, 2048], BF16, "rounded3", "codes10")
-        codes3, scales3 = new_codes("3", 512)
-        interleave(nc.scalar.copy, rounded3[:, 0:512], LOW, 512, 128)
-        scatter(0, copy_out(p20, 256, "v20")[:], 256, 512)
-        scatter(1, copy_out(p21, 256, "v21")[:], 256, 512)
-        interleave(nc.scalar.copy, rounded3[:, 512:1024], LOW, 640, 128)
-        interleave(nc.scalar.copy, rounded3[:, 1024:2048], HIGH, 512, 256)
-        v22 = copy_out(p22, 512, "v22", raw_name(HIGH, 512))
-        quantize(codes3[:], scales3[:], rounded3[:])
-        scatter(2, v22[:, 0:256], 256, 512)
-        scatter(3, v22[:, 256:512], 256, 512)
-        p30 = multiply("p30", "bank1", [0, 1], halves(codes3, scales3))
-        last = [psum.tile([P, 512], F32, name="last%d" % b, tag="bank%d" % b) for b in (2, 3)]
+        rounded, codes, scales = new_wide(3, "codes10")
+        round_wide(rounded, 3, LOW, 0, NARROW)
+        scatter_chunk(2, [0], copy_out(first, "values20"))
+        scatter_chunk(2, [1], copy_out(second, "values21"))
+        round_wide(rounded, 3, LOW, NARROW, WIDE)
+        round_wide(rounded, 3, HIGH, 0, WIDE)
+        values = copy_out(others, "values22", raw_name(HIGH, START[3]))
+        quantize(codes[:], scales[:], rounded[:])
+        scatter_chunk(2, [2, 3], values)
+        chunk3 = by_pass(codes, scales)
+        first = multiply(3, [0], chunk3, 1)
+        second = multiply(3, [1], chunk3, 5)
+        joined = {b: psum.tile([P, 2 * WIDE], F32, name="joined%d" % b, tag="bank%d" % b) for b in (2, 3)}
         for b in (2, 3):
-            for a in (LOW, HIGH):
-                one_pass(last[b - 2][:, 0:256], a, b, codes3[:, a * 256 : (a + 1) * 256], scales3[:, a * 256 : (a + 1) * 256])
+            both_passes(joined[b][:, 0:WIDE], b, chunk3)
 
-        rounded4 = sbuf([P, 2048], BF16, "rounded4")
-        codes4, scales4 = new_codes("4", 512)
-        interleave(nc.scalar.copy, rounded4[:, 0:512], LOW, 768, 128)
-        interleave(nc.scalar.copy, rounded4[:, 512:1024], LOW, 896, 128)
-        interleave(nc.scalar.copy, rounded4[:, 1024:2048], HIGH, 768, 256)
-        v30 = copy_out(p30, 512, "v30", raw_name(HIGH, 768))
-        quantize(codes4[:], scales4[:], rounded4[:])
-        scatter(0, v30[:, 0:256], 512, 768)
-        scatter(1, v30[:, 256:512], 512, 768)
-        p40 = multiply("p40", "bank4", [0, 1], halves(codes4, scales4))
-        v40 = copy_out(p40, 512, "v40")
+        rounded, codes, scales = new_wide(4, "codes10")
+        chunk4 = by_pass(codes, scales)
+        round_wide(rounded, 4, LOW, 0, WIDE)
+        values = copy_out(first, "values30")
+        quantize(*chunk4[LOW], rounded[:, 0 : WIDE * PACK])
+        scatter_chunk(3, [0], values)
+        round_wide(rounded, 4, HIGH, 0, WIDE)
+        values = copy_out(second, "values31", raw_name(HIGH, START[4]))
+        quantize(*chunk4[HIGH], rounded[:, WIDE * PACK : 2 * WIDE * PACK])
+        scatter_chunk(3, [1], values)
         for b in (0, 1):
-            scatter(b, v40[:, b * 256 : (b + 1) * 256], 768, J)
+            scatter_chunk(4, [b], copy_out(multiply(4, [b], chunk4, 6 + b), "values4%d" % b))
             store(b)
         for b in (2, 3):
-            for a in (LOW, HIGH):
-                one_pass(last[b - 2][:, 256:512], a, b, codes4[:, a * 256 : (a + 1) * 256], scales4[:, a * 256 : (a + 1) * 256])
-            scatter(b, copy_out(last[b - 2], 512, "v4%d" % b)[:], 512, J)
+            both_passes(joined[b][:, WIDE : 2 * WIDE], b, chunk4)
+            scatter(b, copy_out(joined[b], "values4%d" % b)[:], START[3], J)
             store(b)

@@ -139,14 +139,14 @@ def tile_list_embg_mix_none_kernel(tc, dy, w8_words, w8_scales, w4_words, w4_sca
             nc.vector.memset(windows[b][:].bitcast(I32), 0)
 
         load_dy(LOW, START[0], START[1])
-        load_gains(START[0], START[1])
+        nc.sync.dma_start(offsets[:], offs)
         load_scales(LOW, w8_scales)
         load_dy(HIGH, START[0], START[2])
         nc.sync.dma_start(out=w8[:].bitcast(I32), in_=w8_words[0].rearrange("p n t -> p (n t)").bitcast(I32))
         nc.sync.dma_start(out=w4[:].bitcast(I32), in_=w4_words[0].bitcast(I32))
         load_scales(HIGH, w4_scales)
+        load_gains(START[0], START[1])
         load_dy(LOW, START[1], START[2])
-        nc.sync.dma_start(offsets[:], offs)
         load_dy(LOW, START[2], START[2] + NARROW)
         load_gains(START[1], START[2])
         load_dy(LOW, START[2] + NARROW, START[3])
@@ -172,7 +172,11 @@ def tile_list_embg_mix_none_kernel(tc, dy, w8_words, w8_scales, w4_words, w4_sca
         scatter_chunk(0, [1], copy_out(second, "values01"))
 
         chunk1 = [prepare_narrow(LOW, 1, nc.scalar.copy, "codes10"), high1]
-        scatter_chunk(0, [2, 3], copy_out(others, "values02", raw_name(LOW, START[1])))
+        values = sbuf([P, 2 * NARROW], F32, "values02", raw_name(LOW, START[1]))
+        for i, b in enumerate((2, 3)):
+            columns = slice(i * NARROW, (i + 1) * NARROW)
+            nc.scalar.copy(out=values[:, columns], in_=others[:, columns])
+            scatter(b, values[:, columns], START[0], START[1])
         first = multiply(1, [0], chunk1, 0)
         second = multiply(1, [1], chunk1, 1)
         others = multiply(1, [2, 3], chunk1, 3)

from contextlib import ExitStack

import concourse.mybir as mybir

K, N, T, J = 1024, 512, 2048, 1024
FLOPS = 2 * K * N * J

F32 = mybir.dt.float32
BF16 = mybir.dt.bfloat16
I32 = mybir.dt.int32
U32 = mybir.dt.uint32
U16 = mybir.dt.uint16
U8 = mybir.dt.uint8
E4M3 = mybir.dt.float8_e4m3fn_x4
E5M2 = mybir.dt.float8_e5m2_x4
E2M1 = mybir.dt.float4_e2m1fn_x4
MULT = mybir.AluOpType.mult

P = 128
PACK = 4
K_PASS = P * PACK
GROUPS = N // P
LIST_ROWS = 16
LOW, HIGH = 0, 1
NARROW = 128
WIDE = 256
START = [0, NARROW, 2 * NARROW, 2 * NARROW + WIDE, 2 * NARROW + 2 * WIDE, J]
VECTOR_ZEROES_3 = 448


def tile_list_embg_mix_none_kernel(tc, dy, w8_words, w8_scales, w4_words, w4_scales, wgo, offs, out):
    nc = tc.nc
    with ExitStack() as ctx:
        keep = ctx.enter_context(tc.tile_pool(name="keep", bufs=1))
        psum = ctx.enter_context(tc.psum_pool(name="psum", bufs=1))

        def sbuf(shape, dtype, name, on=None):
            return keep.tile(shape, dtype, name=name, tag=on or name, align_bytes=64)

        offsets = keep.tile([P, J // LIST_ROWS], U16, name="offsets")
        w_scales = sbuf([P, 2 * N], U8, "w_scales")
        w8 = sbuf([P, N], U32, "w8")
        w4 = sbuf([P, 2 * N], U8, "w4")
        gains = sbuf([P, J], F32, "gains")
        windows = []
        raw = {}

        def raw_name(a, j0):
            return "raw%d_%d" % (a, j0)

        def load_dy(a, j0, j1):
            tile = sbuf([P, PACK, j1 - j0], F32, raw_name(a, j0))
            rows = dy[a * K_PASS : (a + 1) * K_PASS, j0:j1]
            nc.sync.dma_start(out=tile[:], in_=rows.rearrange("(p t) j -> p t j", t=PACK))
            for j in range(j0, j1, NARROW):
                raw[a, j] = (tile, j - j0)

        def load_scales(a, dram):
            for q in range(4):
                nc.sync.dma_start(
                    out=w_scales[32 * q : 32 * q + 4, a * N : (a + 1) * N].bitcast(I32),
                    in_=dram[0, 4 * q : 4 * q + 4, :].bitcast(I32),
                )

        def load_gains(j0, j1):
            nc.sync.dma_start(out=gains[:, j0:j1], in_=wgo[:, j0:j1])

        def interleave(engine_copy, rounded, a, j0, width):
            tile, c0 = raw[a, j0]
            engine_copy(
                out=rounded.rearrange("p (c i t) -> p c t i", i=4, t=PACK),
                in_=tile[:, :, c0 : c0 + width].rearrange("p t (c i) -> p c t i", i=4),
            )

        def quantize(codes, scales, rounded):
            nc.vector.quantize_mx(out=codes.bitcast(E5M2), scales=scales, in_=rounded)

        def prepare_narrow(a, c, engine_copy, on=None):
            rounded = sbuf([P, NARROW * PACK], BF16, "rounded%d%d" % (a, c), on)
            codes = sbuf([P, NARROW], U32, "codes%d%d" % (a, c))
            scales = sbuf([P, NARROW], U8, "scales%d%d" % (a, c))
            interleave(engine_copy, rounded[:], a, START[c], NARROW)
            quantize(codes[:], scales[:], rounded[:])
            return codes[:], scales[:]

        def new_wide(c, on=None):
            rounded = sbuf([P, 2 * WIDE * PACK], BF16, "rounded%d" % c, on)
            return rounded, sbuf([P, 2 * WIDE], U32, "codes%d" % c), sbuf([P, 2 * WIDE], U8, "scales%d" % c)

        def round_wide(rounded, c, a, i0, i1):
            piece = rounded[:, (a * WIDE + i0) * PACK : (a * WIDE + i1) * PACK]
            interleave(nc.scalar.copy, piece, a, START[c] + i0, i1 - i0)

        def by_pass(codes, scales):
            return [(codes[:, a * WIDE : (a + 1) * WIDE], scales[:, a * WIDE : (a + 1) * WIDE]) for a in (LOW, HIGH)]

        def both_passes(product, b, operands):
            n0, n1 = b * P, (b + 1) * P
            weights = [w8[:, n0:n1].bitcast(E4M3), w4[:, 2 * n0 : 2 * n1].bitcast(E2M1)]
            for a in (LOW, HIGH):
                codes, scales = operands[a]
                nc.tensor.matmul_mx(
                    out=product,
                    lhsT=weights[a],
                    lhsT_scale=w_scales[:, a * N + n0 : a * N + n1],
                    rhs=codes.bitcast(E5M2),
                    rhs_scale=scales,
                    start=a == LOW,
                    stop=a == HIGH,
                )

        def multiply(c, groups, operands, bank):
            width = START[c + 1] - START[c]
            products = psum.tile([P, len(groups) * width], F32, name="product%d%d" % (c, groups[0]), tag="bank%d" % bank)
            for i, b in enumerate(groups):
                both_passes(products[:, i * width : (i + 1) * width], b, operands)
            return products

        def copy_out(products, name, on=None):
            values = sbuf([P, products.shape[1]], F32, name, on)
            nc.scalar.copy(out=values[:], in_=products[:])
            return values

        def scatter(b, values, j0, j1):
            places = windows[b][:].indirect(offsets[:, j0 // LIST_ROWS : j1 // LIST_ROWS])
            nc.vector.tensor_tensor(places, values, gains[:, j0:j1], MULT)

        def scatter_chunk(c, groups, values):
            width = START[c + 1] - START[c]
            for i, b in enumerate(groups):
                scatter(b, values[:, i * width : (i + 1) * width], START[c], START[c + 1])

        def store(b):
            for c0, c1 in ((0, T // 2), (T // 2, T)) if b == GROUPS - 1 else ((0, T),):
                nc.sync.dma_start(out=out[b * P : (b + 1) * P, c0:c1], in_=windows[b][:, c0:c1])

        for b in range(GROUPS - 1):
            windows.append(sbuf([P, T], F32, "window%d" % b))
            nc.vector.memset(windows[b][:].bitcast(I32), 0)

        load_dy(LOW, START[0], START[1])
        nc.sync.dma_start(offsets[:], offs)
        load_scales(LOW, w8_scales)
        load_dy(HIGH, START[0], START[2])
        nc.sync.dma_start(out=w8[:].bitcast(I32), in_=w8_words[0].rearrange("p n t -> p (n t)").bitcast(I32))
        nc.sync.dma_start(out=w4[:].bitcast(I32), in_=w4_words[0].bitcast(I32))
        load_scales(HIGH, w4_scales)
        load_gains(START[0], START[1])
        load_dy(LOW, START[1], START[2])
        load_dy(LOW, START[2], START[2] + NARROW)
        load_gains(START[1], START[2])
        load_dy(LOW, START[2] + NARROW, START[3])
        load_dy(HIGH, START[2], START[3])
        load_dy(LOW, START[3], START[4])
        load_gains(START[2], START[3])
        load_dy(HIGH, START[3], START[4])
        load_dy(LOW, START[4], J)
        load_dy(HIGH, START[4], J)
        load_gains(START[3], J)

        low0 = prepare_narrow(LOW, 0, nc.scalar.copy)
        chunk0 = [low0, prepare_narrow(HIGH, 0, nc.vector.tensor_copy)]
        high1 = prepare_narrow(HIGH, 1, nc.scalar.copy)
        windows.append(sbuf([P, T], F32, "window3", "rounded11"))
        nc.vector.memset(windows[3][:, 0 : VECTOR_ZEROES_3 - 1].bitcast(I32), 0)
        nc.gpsimd.memset(windows[3][:, VECTOR_ZEROES_3:T].bitcast(I32), 0)
        nc.vector.memset(windows[3][:, VECTOR_ZEROES_3 - 1 : VECTOR_ZEROES_3].bitcast(I32), 0)
        first = multiply(0, [0], chunk0, 0)
        second = multiply(0, [1], chunk0, 1)
        others = multiply(0, [2, 3], chunk0, 2)
        scatter_chunk(0, [0], copy_out(first, "values00"))
        scatter_chunk(0, [1], copy_out(second, "values01"))

        chunk1 = [prepare_narrow(LOW, 1, nc.scalar.copy, "codes10"), high1]
        values = sbuf([P, 2 * NARROW], F32, "values02", raw_name(LOW, START[1]))
        for i, b in enumerate((2, 3)):
            columns = slice(i * NARROW, (i + 1) * NARROW)
            nc.scalar.copy(out=values[:, columns], in_=others[:, columns])
            scatter(b, values[:, columns], START[0], START[1])
        first = multiply(1, [0], chunk1, 0)
        second = multiply(1, [1], chunk1, 1)
        others = multiply(1, [2, 3], chunk1, 3)

        rounded, codes, scales = new_wide(2, "codes10")
        round_wide(rounded, 2, LOW, 0, NARROW)
        scatter_chunk(1, [0], copy_out(first, "values10", raw_name(LOW, START[2])))
        scatter_chunk(1, [1], copy_out(second, "values11"))
        round_wide(rounded, 2, LOW, NARROW, WIDE)
        round_wide(rounded, 2, HIGH, 0, WIDE)
        values = copy_out(others, "values12", raw_name(HIGH, START[2]))
        chunk2 = by_pass(codes, scales)
        for a in (LOW, HIGH):
            quantize(*chunk2[a], rounded[:, a * WIDE * PACK : (a + 1) * WIDE * PACK])
        scatter_chunk(1, [2, 3], values)
        first = multiply(2, [0], chunk2, 6)
        second = multiply(2, [1], chunk2, 7)
        others = multiply(2, [2, 3], chunk2, 0)

        rounded, codes, scales = new_wide(3, "codes10")
        round_wide(rounded, 3, LOW, 0, NARROW)
        scatter_chunk(2, [0], copy_out(first, "values20"))
        scatter_chunk(2, [1], copy_out(second, "values21"))
        round_wide(rounded, 3, LOW, NARROW, WIDE)
        round_wide(rounded, 3, HIGH, 0, WIDE)
        values = copy_out(others, "values22", raw_name(HIGH, START[3]))
        quantize(codes[:], scales[:], rounded[:])
        scatter_chunk(2, [2, 3], values)
        chunk3 = by_pass(codes, scales)
        first = multiply(3, [0], chunk3, 1)
        second = multiply(3, [1], chunk3, 5)
        joined = {b: psum.tile([P, 2 * WIDE], F32, name="joined%d" % b, tag="bank%d" % b) for b in (2, 3)}
        for b in (2, 3):
            both_passes(joined[b][:, 0:WIDE], b, chunk3)

        rounded, codes, scales = new_wide(4, "codes10")
        chunk4 = by_pass(codes, scales)
        round_wide(rounded, 4, LOW, 0, WIDE)
        values = copy_out(first, "values30")
        quantize(*chunk4[LOW], rounded[:, 0 : WIDE * PACK])
        scatter_chunk(3, [0], values)
        round_wide(rounded, 4, HIGH, 0, WIDE)
        values = copy_out(second, "values31", raw_name(HIGH, START[4]))
        quantize(*chunk4[HIGH], rounded[:, WIDE * PACK : 2 * WIDE * PACK])
        scatter_chunk(3, [1], values)
        for b in (0, 1):
            scatter_chunk(4, [b], copy_out(multiply(4, [b], chunk4, 6 + b), "values4%d" % b))
            store(b)
        for b in (2, 3):
            both_passes(joined[b][:, WIDE : 2 * WIDE], b, chunk4)
            scatter(b, copy_out(joined[b], "values4%d" % b)[:], START[3], J)
            store(b)
